import numpy as np
import ml_dtypes


def mxq(x, axis, fmt="e4m3"):
    dtype, down = {"e4m3": (ml_dtypes.float8_e4m3fn, 7), "e5m2": (ml_dtypes.float8_e5m2, 14)}[fmt]
    v = np.moveaxis(np.asarray(x, np.float32).astype(ml_dtypes.bfloat16).astype(np.float64), axis, -1)
    blocks = v.reshape(v.shape[:-1] + (-1, 32))
    amax = np.abs(blocks).max(-1, keepdims=True)
    byte = np.maximum(np.where(amax > 0, np.frexp(amax)[1] - 1 + 127, 0) - down, 1)
    scale = np.exp2(byte - 127.0)
    codes = (blocks / scale).astype(np.float32).astype(dtype).astype(np.float64)
    return np.moveaxis((codes * scale).reshape(v.shape), -1, axis)


WIDE = False


def mx_kscale(k):
    if not WIDE:
        return np.ones(k)
    levels = np.array([10, -10, 5, -5, 0])
    if k % 512:
        return np.exp2(np.random.permutation(np.resize(levels, k // 32))).repeat(32)
    a = np.empty((k // 512, 16))
    for p in range(k // 512):
        a[p, :8] = np.random.permutation(np.resize(levels, 8))
        for g in range(8):
            far = levels[np.abs(levels - a[p, g]) >= 10]
            a[p, g + 8] = far[np.random.randint(len(far))]
    return np.exp2(a.ravel()).repeat(32)


def f64(x):
    return np.asarray(x).astype(np.float64)


def striped(idx):
    return np.tile(idx.reshape(-1, 16).T, (8, 1)).astype(np.uint16)


def unstriped(offs):
    return offs[:16].T.reshape(-1).astype(np.int64)


E2M1 = np.array([0.0, 0.5, 1.0, 1.5, 2.0, 3.0, 4.0, 6.0, -0.0, -0.5, -1.0, -1.5, -2.0, -3.0, -4.0, -6.0])


def pack_weight(w, fmt):
    k, n = w.shape
    w = f64(np.asarray(w, np.float32).astype(ml_dtypes.bfloat16)).reshape(k // 32, 32, n)
    amax = np.abs(w).max(1)
    if fmt == "e4m3":
        byte = np.frexp(amax)[1] - 1 + 127 - 7
    else:
        mant, ex = np.frexp(amax / 6.0)
        byte = np.where(mant > 0.5, ex, ex - 1) + 127
    byte = np.clip(np.where(amax > 0, byte, 1), 1, 254)
    scaled = (w * np.exp2(127.0 - byte)[:, None, :]).reshape(k, n).astype(np.float32)
    by_word = np.ascontiguousarray(scaled.reshape(k // 512, 128, 4, n).transpose(0, 1, 3, 2))
    if fmt == "e4m3":
        words = by_word.astype(ml_dtypes.float8_e4m3fn).view(np.uint8)
    else:
        c = by_word.astype(ml_dtypes.float4_e2m1fn).view(np.uint8) & 0xF
        words = (c[..., 0::2] | (c[..., 1::2] << 4)).reshape(k // 512, 128, 2 * n)
    return np.ascontiguousarray(words), np.ascontiguousarray(byte.astype(np.uint8).reshape(k // 512, 16, n))


def unpack_weight(words, scales, fmt):
    g, _, n = scales.shape
    words = np.ascontiguousarray(words).reshape(g, 128, n, -1)
    if fmt == "e4m3":
        vals = words.view(ml_dtypes.float8_e4m3fn).astype(np.float64)
    else:
        nib = np.empty((g, 128, n, 4), np.uint8)
        nib[..., 0::2] = words & 0xF
        nib[..., 1::2] = words >> 4
        vals = E2M1[nib]
    vals = vals * np.repeat(np.exp2(scales.astype(np.float64) - 127.0), 8, axis=1)[..., None]
    return vals.transpose(0, 1, 3, 2).reshape(g * 512, n)


def d_relu2(v):
    return 2.0 * np.maximum(v, 0.0)


K, T, E, C, H, N = 128, 512, 4, 256, 512, 512


def by_expert(wq, xq):
    return np.concatenate([wq[e].T @ xq[:, e * C:(e + 1) * C] for e in range(E)], axis=1)


def setup_inputs():
    n = np.random.standard_normal
    v = mx_kscale(N)
    u = mx_kscale(H)
    first = np.random.permutation(np.repeat(np.arange(E), T // E))
    second = (first + 1 + np.random.permutation(np.repeat(np.arange(E - 1), -(-T // (E - 1)))[:T])) % E
    while np.bincount(second, minlength=E).max() != T // E:
        load = np.bincount(second, minlength=E); hi, lo = int(load.argmax()), int(load.argmin())
        t = np.flatnonzero((second == hi) & (first != lo))[0]; second[t] = lo
    slot_token = np.empty(E * C, np.int64); pos = np.empty((2, T), np.int64); fill = np.zeros(E, np.int64)
    place = np.stack([np.random.permutation(C) for _ in range(E)])
    for r, deal in enumerate((first, second)):
        for t in np.random.permutation(T):
            e = deal[t]; j = e * C + place[e, fill[e]]; fill[e] += 1; slot_token[j] = t; pos[r, t] = j
    g = np.random.uniform(0.2, 0.8, T)
    dy = pack_weight(n((N, T)) * v[:, None], "e4m3")
    w2t = [pack_weight(m, "e2m1") for m in n((E, N, H)) / np.sqrt(N) / v[None, :, None] * u]
    w1t = pack_weight(n((H, K)) / np.sqrt(H) / u[:, None], "e4m3")
    return {
        "dy_words": dy[0],
        "dy_scales": dy[1],
        "w2t_words": np.stack([m[0] for m in w2t]),
        "w2t_scales": np.stack([m[1] for m in w2t]),
        "w1t_words": w1t[0],
        "w1t_scales": w1t[1],
        "a": (n((H, T))).astype(np.float32),
        "gate": np.stack([np.tile(g, (128, 1)), np.tile(1.0 - g, (128, 1))]).astype(np.float32),
        "offs": striped(slot_token),
        "pos1": striped(pos[0]),
        "pos2": striped(pos[1]),
    }


def reference(dy_words, dy_scales, w2t_words, w2t_scales, w1t_words, w1t_scales, a, gate, offs, pos1, pos2):
    w2t = np.stack([unpack_weight(w2t_words[e], w2t_scales[e], "e2m1") for e in range(E)])
    w1t = unpack_weight(w1t_words, w1t_scales, "e4m3")
    idx = unstriped(offs)
    gq = unpack_weight(dy_words, dy_scales, "e4m3")[:, idx]
    y = by_expert(w2t, gq)
    dh = sum(f64(gate[r, :1]) * y[:, unstriped(p)] for r, p in enumerate((pos1, pos2)))
    return w1t.T @ mxq(dh * d_relu2(f64(a)), 0, "e4m3")

@@ -1,0 +1,210 @@
+from contextlib import ExitStack
+
+import concourse.mybir as mybir
+from concourse.masks import make_identity
+
+K, T, E, C, H, N = 128, 512, 4, 256, 512, 512
+S = E * C
+P = 128
+FLOPS = 2 * N * H * S + 2 * H * K * T
+
+F32 = mybir.dt.float32
+BF16 = mybir.dt.bfloat16
+I32 = mybir.dt.int32
+U32 = mybir.dt.uint32
+U16 = mybir.dt.uint16
+U8 = mybir.dt.uint8
+FP8X4 = mybir.dt.float8_e4m3fn_x4
+FP4X4 = mybir.dt.float4_e2m1fn_x4
+MULT = mybir.AluOpType.mult
+RELU = mybir.ActivationFunctionType.Relu
+COPY = mybir.ActivationFunctionType.Copy
+
+PIECES = ((0, 256), (256, 128), (384, 128))
+
+
+def tile_moe_sub_relu2_kernel(
+    tc, dy_words, dy_scales, w2t_words, w2t_scales, w1t_words, w1t_scales, a, gate, offs, pos1, pos2, out
+):
+    nc = tc.nc
+    with ExitStack() as ctx:
+        held = ctx.enter_context(tc.tile_pool(name="held", bufs=1))
+        ring = ctx.enter_context(tc.tile_pool(name="ring", bufs=4))
+        psum = ctx.enter_context(tc.psum_pool(name="psum", bufs=1))
+
+        def bank(b, shape, name):
+            return psum.tile(shape, F32, name=name, tag="bank%d" % b)
+
+        offs_t = held.tile([P, S // 16], U16, name="offs_t")
+        pos_t = [held.tile([P, T // 16], U16, name="pos_t%d" % r) for r in range(2)]
+        dyw = held.tile([P, T], I32, name="dyw", align_bytes=64)
+        dys = held.tile([P, T], U8, name="dys", align_bytes=64)
+        w2w = held.tile([P, E, 2 * H], U8, name="w2w", align_bytes=64)
+        w2s = held.tile([P, E, H], U8, name="w2s", align_bytes=64)
+        w1w = held.tile([P, K], I32, name="w1w", align_bytes=64)
+        w1s = held.tile([P, K], U8, name="w1s", align_bytes=64)
+        gate_t = held.tile([P, 2, T], F32, name="gate_t")
+        a_t = held.tile([P, 4, T], F32, name="a_t")
+        ident = held.tile([P, P], F32, name="ident")
+        warm = held.tile([P, 8], F32, name="warm")
+        warm2 = held.tile([P, 8], F32, name="warm2")
+
+        nc.sync.dma_start(offs_t[:], offs)
+        nc.scalar.dma_start(dyw[:], dy_words[0].rearrange("p t d -> p (t d)").bitcast(I32))
+        nc.vector.memset(dys[:].bitcast(I32), 0)
+        nc.vector.memset(w2s[:].rearrange("p e c -> p (e c)").bitcast(I32), 0)
+        nc.vector.memset(w1s[:].bitcast(I32), 0)
+        nc.gpsimd.memset(warm[:], 0.0)
+        nc.scalar.activation(warm2[:], warm[:], RELU)
+        make_identity(nc, ident[:])
+        for q in range(4):
+            nc.sync.dma_start(dys[32 * q : 32 * q + 4, :].bitcast(I32), dy_scales[0, 4 * q : 4 * q + 4, :].bitcast(I32))
+        nc.sync.dma_start(w2w[:].bitcast(I32), w2t_words[:, 0].rearrange("e p c -> p e c").bitcast(I32))
+        for q in range(4):
+            nc.sync.dma_start(
+                w2s[32 * q : 32 * q + 4].bitcast(I32),
+                w2t_scales[:, 0, 4 * q : 4 * q + 4, :].rearrange("e r c -> r e c").bitcast(I32),
+            )
+        nc.sync.dma_start(pos_t[0][:], pos1)
+        nc.sync.dma_start(pos_t[1][:], pos2)
+        nc.sync.dma_start(gate_t[:], gate.rearrange("r p t -> p r t"))
+        nc.sync.dma_start(a_t[:], a.rearrange("(j p) t -> p j t", p=P))
+        nc.sync.dma_start(w1w[:], w1t_words[0].rearrange("p k d -> p (k d)").bitcast(I32))
+        for q in range(4):
+            nc.sync.dma_start(w1s[32 * q : 32 * q + 4, :].bitcast(I32), w1t_scales[0, 4 * q : 4 * q + 4, :].bitcast(I32))
+
+        gw = [held.tile([P, C], U32, name="gw%d" % e, align_bytes=64) for e in range(E)]
+        gs = [held.tile([P, C], U8, name="gs%d" % e, align_bytes=64) for e in range(E)]
+        y = [held.tile([P, S], F32, name="y%d" % j) for j in range(4)]
+
+        def gather_words(e):
+            nc.vector.tensor_copy(gw[e][:], dyw[:].bitcast(U32).indirect(offs_t[:, 16 * e : 16 * (e + 1)]))
+
+        def gather_scales(e):
+            nc.vector.tensor_copy(gs[e][:], dys[:].indirect(offs_t[:, 16 * e : 16 * (e + 1)]))
+
+        def expert_mm(acc, e, j):
+            nc.tensor.matmul_mx(
+                out=acc[:, (e % 2) * C : (e % 2 + 1) * C],
+                lhsT=w2w[:, e, 2 * P * j : 2 * P * (j + 1)].bitcast(FP4X4),
+                lhsT_scale=w2s[:, e, P * j : P * (j + 1)],
+                rhs=gw[e][:].bitcast(FP8X4),
+                rhs_scale=gs[e][:],
+                start=True,
+                stop=True,
+            )
+
+        gather_words(0)
+        gather_words(1)
+        gather_scales(0)
+        gather_scales(1)
+        acc0 = [bank(j, [P, 2 * C], "acc0_%d" % j) for j in range(4)]
+        for j in range(4):
+            expert_mm(acc0[j], 0, j)
+            expert_mm(acc0[j], 1, j)
+            nc.scalar.copy(y[j][:, 0 : 2 * C], acc0[j][:])
+        gather_words(2)
+        gather_scales(2)
+        gather_words(3)
+        gather_scales(3)
+        acc1 = [bank(4 + j, [P, 2 * C], "acc1_%d" % j) for j in range(4)]
+        expert_mm(acc1[0], 2, 0)
+        nc.scalar.copy(y[0][:, 2 * C : 3 * C], acc1[0][:, 0:C])
+        for j in range(1, 4):
+            expert_mm(acc1[j], 2, j)
+        expert_mm(acc1[0], 3, 0)
+        nc.scalar.copy(y[0][:, 3 * C : 4 * C], acc1[0][:, C : 2 * C])
+        for j in range(1, 4):
+            expert_mm(acc1[j], 3, j)
+            nc.scalar.copy(y[j][:, 2 * C : 4 * C], acc1[j][:])
+
+        rt = [held.tile([P, 2, P, 2], F32, name="rt%d" % tt) for tt in range(4)]
+
+        def slope(tt):
+            at = bank(7 - tt % 2, [P, H], "at%d" % tt)
+            for j in range(4):
+                nc.tensor.transpose(at[:, P * j : P * (j + 1)], a_t[:, j, P * tt : P * (tt + 1)], ident[:])
+            nc.scalar.activation(rt[tt][:], at[:].rearrange("t (p u e) -> t u p e", u=2, e=2), RELU, scale=2.0)
+
+        for tt in range(4):
+            slope(tt)
+
+        st = [bank(tt, [P, H], "st%d" % tt) for tt in range(4)]
+        st_last = bank(4, [P, P], "st_last")
+        dat = [held.tile([P, 2, P, 2], BF16, name="dat%d" % tt, align_bytes=64) for tt in range(4)]
+
+        def combine(piece, j):
+            t0, n = PIECES[piece]
+            for r in range(2):
+                z = ring.tile([P, n], F32, name="z")
+                nc.vector.tensor_tensor(
+                    z[:], y[j][:].indirect(pos_t[r][:, t0 // 16 : (t0 + n) // 16]), gate_t[:, r, t0 : t0 + n], MULT
+                )
+                for k in range(n // P):
+                    tt = t0 // P + k
+                    dst = st_last[:] if (tt == 3 and j == 3) else st[tt][:, P * j : P * (j + 1)]
+                    nc.tensor.matmul(
+                        dst, z[:, P * k : P * (k + 1)], ident[:], start=(r == 0), stop=(r == 1), is_transpose=True
+                    )
+
+        def times_slope(tt, src, p0, p1):
+            nc.vector.tensor_tensor(
+                dat[tt][:, :, p0:p1, :], src.rearrange("t (p u e) -> t u p e", u=2, e=2), rt[tt][:, :, p0:p1, :], MULT
+            )
+
+        grouped = {}
+
+        def turn_back(piece, b):
+            t0, n = PIECES[piece]
+            m = n // P
+            wt = bank(b, [P, m, 2, P], "wt%d" % piece)
+            for k in range(m):
+                words = dat[t0 // P + k][:].rearrange("t u p e -> t (u p e)").bitcast(F32)
+                for u in range(2):
+                    nc.tensor.transpose(wt[:, k, u, :], words[:, P * u : P * (u + 1)], ident[:])
+            g = held.tile([P, 4 * n], BF16, name="grouped%d" % piece, align_bytes=64)
+            nc.scalar.copy(
+                g[:].bitcast(F32).rearrange("p (k t u) -> p k t u", k=m, u=2), wt[:].rearrange("p k u t -> p k t u")
+            )
+            grouped[piece] = g
+
+        def finish(piece, b):
+            t0, n = PIECES[piece]
+            codes = held.tile([P, n], U32, name="codes%d" % piece, align_bytes=64)
+            scales = held.tile([P, n], U8, name="scales%d" % piece, align_bytes=64)
+            nc.vector.quantize_mx(out=codes[:].bitcast(FP8X4), scales=scales[:], in_=grouped[piece][:])
+            acc = bank(b, [P, n], "acc_out%d" % piece)
+            nc.tensor.matmul_mx(
+                out=acc[:],
+                lhsT=w1w[:].bitcast(FP8X4),
+                lhsT_scale=w1s[:],
+                rhs=codes[:].bitcast(FP8X4),
+                rhs_scale=scales[:],
+                start=True,
+                stop=True,
+            )
+            res = held.tile([P, n], F32, name="res%d" % piece)
+            nc.scalar.copy(res[:], acc[:])
+            nc.sync.dma_start(out[:, t0 : t0 + n], res[:])
+
+        for j in range(4):
+            combine(0, j)
+        combine(1, 0)
+        times_slope(0, st[0][:], 0, P)
+        combine(1, 1)
+        times_slope(1, st[1][:], 0, P)
+        turn_back(0, 5)
+        combine(1, 2)
+        combine(1, 3)
+        combine(2, 0)
+        finish(0, 6)
+        times_slope(2, st[2][:], 0, P)
+        turn_back(1, 0)
+        combine(2, 1)
+        combine(2, 2)
+        finish(1, 7)
+        combine(2, 3)
+        times_slope(3, st[3][:, 0 : 3 * P], 0, 96)
+        times_slope(3, st_last[:], 96, P)
+        turn_back(2, 1)
+        finish(2, 5)

@@ -17,10 +17,13 @@ U8 = mybir.dt.uint8
 FP8X4 = mybir.dt.float8_e4m3fn_x4
 FP4X4 = mybir.dt.float4_e2m1fn_x4
 MULT = mybir.AluOpType.mult
+MAX = mybir.AluOpType.max
 RELU = mybir.ActivationFunctionType.Relu
 COPY = mybir.ActivationFunctionType.Copy
 
-PIECES = ((0, 256), (256, 128), (384, 128))
+PIECES = ((0, 384), (384, 128))
+GROUPS = ((0, 256), (256, 128), (384, 128))
+REUSE = {(1, 1, 0): "rt0", (1, 1, 1): "rt1", (1, 3, 1): "grouped0"}
 
 
 def tile_moe_sub_relu2_kernel(
@@ -29,7 +32,6 @@ def tile_moe_sub_relu2_kernel(
     nc = tc.nc
     with ExitStack() as ctx:
         held = ctx.enter_context(tc.tile_pool(name="held", bufs=1))
-        ring = ctx.enter_context(tc.tile_pool(name="ring", bufs=4))
         psum = ctx.enter_context(tc.psum_pool(name="psum", bufs=1))
 
         def bank(b, shape, name):
@@ -44,31 +46,37 @@ def tile_moe_sub_relu2_kernel(
         w1w = held.tile([P, K], I32, name="w1w", align_bytes=64)
         w1s = held.tile([P, K], U8, name="w1s", align_bytes=64)
         gate_t = held.tile([P, 2, T], F32, name="gate_t")
-        a_t = held.tile([P, 4, T], F32, name="a_t")
+        a_t = held.tile([P, 4, 3 * P], F32, name="a_t")
+        a_last = held.tile([P, 4, P], F32, name="a_last")
+        gl = [held.tile([P, 4, P], F32, name="gl%d" % r, tag="gl%d" % r, align_bytes=64) for r in range(2)]
         ident = held.tile([P, P], F32, name="ident")
         warm = held.tile([P, 8], F32, name="warm")
         warm2 = held.tile([P, 8], F32, name="warm2")
 
         nc.sync.dma_start(offs_t[:], offs)
+        for q in range(4):
+            (nc.sync if q < 2 else nc.scalar).dma_start(
+                dys[32 * q : 32 * (q + 1), :].bitcast(I32),
+                dy_scales[0, 4 * q : 4 * q + 4, :].bitcast(I32).unsqueeze(0).to_broadcast([8, 4, T // 4]),
+            )
         nc.scalar.dma_start(dyw[:], dy_words[0].rearrange("p t d -> p (t d)").bitcast(I32))
-        nc.vector.memset(dys[:].bitcast(I32), 0)
         nc.vector.memset(w2s[:].rearrange("p e c -> p (e c)").bitcast(I32), 0)
-        nc.vector.memset(w1s[:].bitcast(I32), 0)
         nc.gpsimd.memset(warm[:], 0.0)
+        nc.gpsimd.memset(w1s[:].bitcast(I32), 0)
         nc.scalar.activation(warm2[:], warm[:], RELU)
         make_identity(nc, ident[:])
-        for q in range(4):
-            nc.sync.dma_start(dys[32 * q : 32 * q + 4, :].bitcast(I32), dy_scales[0, 4 * q : 4 * q + 4, :].bitcast(I32))
+        a_rows = a.rearrange("(j p) t -> p j t", p=P)
+        nc.sync.dma_start(pos_t[0][:], pos1)
         nc.sync.dma_start(w2w[:].bitcast(I32), w2t_words[:, 0].rearrange("e p c -> p e c").bitcast(I32))
         for q in range(4):
             nc.sync.dma_start(
                 w2s[32 * q : 32 * q + 4].bitcast(I32),
                 w2t_scales[:, 0, 4 * q : 4 * q + 4, :].rearrange("e r c -> r e c").bitcast(I32),
             )
-        nc.sync.dma_start(pos_t[0][:], pos1)
-        nc.sync.dma_start(pos_t[1][:], pos2)
         nc.sync.dma_start(gate_t[:], gate.rearrange("r p t -> p r t"))
-        nc.sync.dma_start(a_t[:], a.rearrange("(j p) t -> p j t", p=P))
+        nc.sync.dma_start(a_last[:], a_rows[:, :, 3 * P : T])
+        nc.sync.dma_start(pos_t[1][:], pos2)
+        nc.sync.dma_start(a_t[:], a_rows[:, :, 0 : 3 * P])
         nc.sync.dma_start(w1w[:], w1t_words[0].rearrange("p k d -> p (k d)").bitcast(I32))
         for q in range(4):
             nc.sync.dma_start(w1s[32 * q : 32 * q + 4, :].bitcast(I32), w1t_scales[0, 4 * q : 4 * q + 4, :].bitcast(I32))
@@ -94,31 +102,42 @@ def tile_moe_sub_relu2_kernel(
                 stop=True,
             )
 
-        gather_words(0)
-        gather_words(1)
         gather_scales(0)
         gather_scales(1)
-        acc0 = [bank(j, [P, 2 * C], "acc0_%d" % j) for j in range(4)]
-        for j in range(4):
-            expert_mm(acc0[j], 0, j)
-            expert_mm(acc0[j], 1, j)
-            nc.scalar.copy(y[j][:, 0 : 2 * C], acc0[j][:])
-        gather_words(2)
+        gather_words(0)
+        gather_words(1)
         gather_scales(2)
-        gather_words(3)
+        gather_words(2)
         gather_scales(3)
-        acc1 = [bank(4 + j, [P, 2 * C], "acc1_%d" % j) for j in range(4)]
-        expert_mm(acc1[0], 2, 0)
-        nc.scalar.copy(y[0][:, 2 * C : 3 * C], acc1[0][:, 0:C])
+        gather_words(3)
+        for r in range(2):
+            nc.vector.scalar_tensor_tensor(
+                gl[r][:], a_last[:], 0.0, gate_t[:, r, 3 * P : T].unsqueeze(1).to_broadcast([P, 4, P]), MAX, MULT
+            )
+        low = [bank(j, [P, 2 * C], "low%d" % j) for j in range(4)]
+        expert_mm(low[0], 0, 0)
+        expert_mm(low[0], 1, 0)
+        nc.scalar.copy(y[0][:, 0 : 2 * C], low[0][:])
+        expert_mm(low[1], 0, 1)
+        expert_mm(low[1], 1, 1)
+        nc.scalar.copy(y[1][:, 0 : 2 * C], low[1][:])
+        third = bank(4, [P, 2 * C], "third")
+        expert_mm(third, 2, 0)
+        nc.scalar.copy(y[0][:, 2 * C : 3 * C], third[:, 0:C])
+        fourth = bank(5, [P, 2 * C], "fourth")
+        expert_mm(fourth, 3, 0)
+        nc.scalar.copy(y[0][:, 3 * C : 4 * C], fourth[:, C : 2 * C])
         for j in range(1, 4):
-            expert_mm(acc1[j], 2, j)
-        expert_mm(acc1[0], 3, 0)
-        nc.scalar.copy(y[0][:, 3 * C : 4 * C], acc1[0][:, C : 2 * C])
-        for j in range(1, 4):
-            expert_mm(acc1[j], 3, j)
-            nc.scalar.copy(y[j][:, 2 * C : 4 * C], acc1[j][:])
+            if j > 1:
+                expert_mm(low[j], 0, j)
+                expert_mm(low[j], 1, j)
+                nc.scalar.copy(y[j][:, 0 : 2 * C], low[j][:])
+            high = bank((6, 7, 4)[j - 1], [P, 2 * C], "high%d" % j)
+            expert_mm(high, 2, j)
+            expert_mm(high, 3, j)
+            nc.scalar.copy(y[j][:, 2 * C : 4 * C], high[:])
 
-        rt = [held.tile([P, 2, P, 2], F32, name="rt%d" % tt) for tt in range(4)]
+        rt = [held.tile([P, 2, P, 2], F32, name="rt%d" % tt, tag="rt%d" % tt, align_bytes=64) for tt in range(3)]
 
         def slope(tt):
             at = bank(7 - tt % 2, [P, H], "at%d" % tt)
@@ -126,20 +145,23 @@ def tile_moe_sub_relu2_kernel(
                 nc.tensor.transpose(at[:, P * j : P * (j + 1)], a_t[:, j, P * tt : P * (tt + 1)], ident[:])
             nc.scalar.activation(rt[tt][:], at[:].rearrange("t (p u e) -> t u p e", u=2, e=2), RELU, scale=2.0)
 
-        for tt in range(4):
+        for tt in range(3):
             slope(tt)
 
         st = [bank(tt, [P, H], "st%d" % tt) for tt in range(4)]
         st_last = bank(4, [P, P], "st_last")
-        dat = [held.tile([P, 2, P, 2], BF16, name="dat%d" % tt, align_bytes=64) for tt in range(4)]
+        dat = {}
+
+        def new_dat(tt, tag):
+            dat[tt] = held.tile([P, 2, P, 2], BF16, name="dat%d" % tt, tag=tag, align_bytes=64)
 
         def combine(piece, j):
             t0, n = PIECES[piece]
             for r in range(2):
-                z = ring.tile([P, n], F32, name="z")
-                nc.vector.tensor_tensor(
-                    z[:], y[j][:].indirect(pos_t[r][:, t0 // 16 : (t0 + n) // 16]), gate_t[:, r, t0 : t0 + n], MULT
-                )
+                own = "z%d_%d_%d" % (piece, j, r)
+                z = held.tile([P, n], F32, name=own, tag=REUSE.get((piece, j, r), own), align_bytes=64)
+                factor = gate_t[:, r, t0 : t0 + n] if piece == 0 else gl[r][:, j, :]
+                nc.vector.tensor_tensor(z[:], y[j][:].indirect(pos_t[r][:, t0 // 16 : (t0 + n) // 16]), factor, MULT)
                 for k in range(n // P):
                     tt = t0 // P + k
                     dst = st_last[:] if (tt == 3 and j == 3) else st[tt][:, P * j : P * (j + 1)]
@@ -152,24 +174,29 @@ def tile_moe_sub_relu2_kernel(
                 dat[tt][:, :, p0:p1, :], src.rearrange("t (p u e) -> t u p e", u=2, e=2), rt[tt][:, :, p0:p1, :], MULT
             )
 
+        def twice(tt, src, p0, p1):
+            nc.scalar.activation(
+                dat[tt][:, :, p0:p1, :], src.rearrange("t (p u e) -> t u p e", u=2, e=2), COPY, scale=2.0
+            )
+
         grouped = {}
 
         def turn_back(piece, b):
-            t0, n = PIECES[piece]
+            t0, n = GROUPS[piece]
             m = n // P
             wt = bank(b, [P, m, 2, P], "wt%d" % piece)
             for k in range(m):
                 words = dat[t0 // P + k][:].rearrange("t u p e -> t (u p e)").bitcast(F32)
                 for u in range(2):
                     nc.tensor.transpose(wt[:, k, u, :], words[:, P * u : P * (u + 1)], ident[:])
-            g = held.tile([P, 4 * n], BF16, name="grouped%d" % piece, align_bytes=64)
+            g = held.tile([P, 4 * n], BF16, name="grouped%d" % piece, tag="grouped%d" % piece, align_bytes=64)
             nc.scalar.copy(
                 g[:].bitcast(F32).rearrange("p (k t u) -> p k t u", k=m, u=2), wt[:].rearrange("p k u t -> p k t u")
             )
             grouped[piece] = g
 
         def finish(piece, b):
-            t0, n = PIECES[piece]
+            t0, n = GROUPS[piece]
             codes = held.tile([P, n], U32, name="codes%d" % piece, align_bytes=64)
             scales = held.tile([P, n], U8, name="scales%d" % piece, align_bytes=64)
             nc.vector.quantize_mx(out=codes[:].bitcast(FP8X4), scales=scales[:], in_=grouped[piece][:])
@@ -190,21 +217,20 @@ def tile_moe_sub_relu2_kernel(
         for j in range(4):
             combine(0, j)
         combine(1, 0)
-        times_slope(0, st[0][:], 0, P)
-        combine(1, 1)
-        times_slope(1, st[1][:], 0, P)
+        for tt in range(2):
+            new_dat(tt, "dat%d" % tt)
+            times_slope(tt, st[tt][:], 0, P)
         turn_back(0, 5)
+        combine(1, 1)
         combine(1, 2)
-        combine(1, 3)
-        combine(2, 0)
+        new_dat(3, "dat3")
+        twice(3, st[3][:, 0 : 3 * P], 0, 96)
         finish(0, 6)
+        combine(1, 3)
+        twice(3, st_last[:], 96, P)
+        new_dat(2, "gl1")
         times_slope(2, st[2][:], 0, P)
         turn_back(1, 0)
-        combine(2, 1)
-        combine(2, 2)
-        finish(1, 7)
-        combine(2, 3)
-        times_slope(3, st[3][:, 0 : 3 * P], 0, 96)
-        times_slope(3, st_last[:], 96, P)
         turn_back(2, 1)
+        finish(1, 7)
         finish(2, 5)

@@ -23,7 +23,7 @@ COPY = mybir.ActivationFunctionType.Copy
 
 PIECES = ((0, 384), (384, 128))
 GROUPS = ((0, 256), (256, 128), (384, 128))
-REUSE = {(1, 1, 0): "rt0", (1, 1, 1): "rt1", (1, 3, 1): "grouped0"}
+REUSE = {(1, 2, 0): "gate0", (1, 2, 1): "gate1", (1, 3, 0): "rt0", (1, 3, 1): "rt1"}
 
 
 def tile_moe_sub_relu2_kernel(
@@ -45,7 +45,7 @@ def tile_moe_sub_relu2_kernel(
         w2s = held.tile([P, E, H], U8, name="w2s", align_bytes=64)
         w1w = held.tile([P, K], I32, name="w1w", align_bytes=64)
         w1s = held.tile([P, K], U8, name="w1s", align_bytes=64)
-        gate_t = held.tile([P, 2, T], F32, name="gate_t")
+        gate_t = [held.tile([P, T], F32, name="gate%d" % r, tag="gate%d" % r, align_bytes=64) for r in range(2)]
         a_t = held.tile([P, 4, 3 * P], F32, name="a_t")
         a_last = held.tile([P, 4, P], F32, name="a_last")
         gl = [held.tile([P, 4, P], F32, name="gl%d" % r, tag="gl%d" % r, align_bytes=64) for r in range(2)]
@@ -73,7 +73,8 @@ def tile_moe_sub_relu2_kernel(
                 w2s[32 * q : 32 * q + 4].bitcast(I32),
                 w2t_scales[:, 0, 4 * q : 4 * q + 4, :].rearrange("e r c -> r e c").bitcast(I32),
             )
-        nc.sync.dma_start(gate_t[:], gate.rearrange("r p t -> p r t"))
+        for r in range(2):
+            nc.sync.dma_start(gate_t[r][:], gate[r])
         nc.sync.dma_start(a_last[:], a_rows[:, :, 3 * P : T])
         nc.sync.dma_start(pos_t[1][:], pos2)
         nc.sync.dma_start(a_t[:], a_rows[:, :, 0 : 3 * P])
@@ -83,21 +84,23 @@ def tile_moe_sub_relu2_kernel(
 
         gw = [held.tile([P, C], U32, name="gw%d" % e, align_bytes=64) for e in range(E)]
         gs = [held.tile([P, C], U8, name="gs%d" % e, align_bytes=64) for e in range(E)]
-        y = [held.tile([P, S], F32, name="y%d" % j) for j in range(4)]
+        y = [held.tile([P, S], F32, name="y%d" % j, tag="y%d" % j, align_bytes=64) for j in range(4)]
 
-        def gather_words(e):
-            nc.vector.tensor_copy(gw[e][:], dyw[:].bitcast(U32).indirect(offs_t[:, 16 * e : 16 * (e + 1)]))
+        def gather_words(e, c0=0, c1=C):
+            nc.vector.tensor_copy(
+                gw[e][:, c0:c1], dyw[:].bitcast(U32).indirect(offs_t[:, (e * C + c0) // 16 : (e * C + c1) // 16])
+            )
 
         def gather_scales(e):
             nc.vector.tensor_copy(gs[e][:], dys[:].indirect(offs_t[:, 16 * e : 16 * (e + 1)]))
 
-        def expert_mm(acc, e, j):
+        def expert_mm(acc, e, j, c0=0, c1=C):
             nc.tensor.matmul_mx(
-                out=acc[:, (e % 2) * C : (e % 2 + 1) * C],
+                out=acc[:, (e % 2) * C + c0 : (e % 2) * C + c1],
                 lhsT=w2w[:, e, 2 * P * j : 2 * P * (j + 1)].bitcast(FP4X4),
                 lhsT_scale=w2s[:, e, P * j : P * (j + 1)],
-                rhs=gw[e][:].bitcast(FP8X4),
-                rhs_scale=gs[e][:],
+                rhs=gw[e][:, c0:c1].bitcast(FP8X4),
+                rhs_scale=gs[e][:, c0:c1],
                 start=True,
                 stop=True,
             )
@@ -109,44 +112,47 @@ def tile_moe_sub_relu2_kernel(
         gather_scales(2)
         gather_words(2)
         gather_scales(3)
-        gather_words(3)
+        gather_words(3, 0, P)
+        gather_words(3, P, C)
         for r in range(2):
             nc.vector.scalar_tensor_tensor(
-                gl[r][:], a_last[:], 0.0, gate_t[:, r, 3 * P : T].unsqueeze(1).to_broadcast([P, 4, P]), MAX, MULT
+                gl[r][:], a_last[:], 0.0, gate_t[r][:, 3 * P : T].unsqueeze(1).to_broadcast([P, 4, P]), MAX, MULT
             )
-        low = [bank(j, [P, 2 * C], "low%d" % j) for j in range(4)]
+        rt = [held.tile([P, 2, P, 2], F32, name="rt%d" % tt, tag="rt%d" % tt, align_bytes=64) for tt in range(3)]
+
+        def slope(tt):
+            at = bank((6, 7, 5)[tt], [P, H], "at%d" % tt)
+            for j in range(4):
+                nc.tensor.transpose(at[:, P * j : P * (j + 1)], a_t[:, j, P * tt : P * (tt + 1)], ident[:])
+            nc.scalar.activation(rt[tt][:], at[:].rearrange("t (p u e) -> t u p e", u=2, e=2), RELU, scale=2.0)
+
+        low = [bank(j, [P, 2 * C], "low%d" % j) for j in range(3)]
         expert_mm(low[0], 0, 0)
         expert_mm(low[0], 1, 0)
         nc.scalar.copy(y[0][:, 0 : 2 * C], low[0][:])
-        expert_mm(low[1], 0, 1)
-        expert_mm(low[1], 1, 1)
-        nc.scalar.copy(y[1][:, 0 : 2 * C], low[1][:])
         third = bank(4, [P, 2 * C], "third")
         expert_mm(third, 2, 0)
         nc.scalar.copy(y[0][:, 2 * C : 3 * C], third[:, 0:C])
-        fourth = bank(5, [P, 2 * C], "fourth")
-        expert_mm(fourth, 3, 0)
-        nc.scalar.copy(y[0][:, 3 * C : 4 * C], fourth[:, C : 2 * C])
+        expert_mm(low[1], 0, 1)
+        for c0, b in ((0, 5), (P, 3)):
+            fourth = bank(b, [P, 2 * C], "fourth%d" % c0)
+            expert_mm(fourth, 3, 0, c0, c0 + P)
+            nc.scalar.copy(y[0][:, 3 * C + c0 : 3 * C + c0 + P], fourth[:, C + c0 : C + c0 + P])
+        low.append(bank(3, [P, 2 * C], "low3"))
         for j in range(1, 4):
+            if j == 3:
+                slope(0)
             if j > 1:
                 expert_mm(low[j], 0, j)
-                expert_mm(low[j], 1, j)
-                nc.scalar.copy(y[j][:, 0 : 2 * C], low[j][:])
+            expert_mm(low[j], 1, j)
+            nc.scalar.copy(y[j][:, 0 : 2 * C], low[j][:])
             high = bank((6, 7, 4)[j - 1], [P, 2 * C], "high%d" % j)
             expert_mm(high, 2, j)
             expert_mm(high, 3, j)
             nc.scalar.copy(y[j][:, 2 * C : 4 * C], high[:])
 
-        rt = [held.tile([P, 2, P, 2], F32, name="rt%d" % tt, tag="rt%d" % tt, align_bytes=64) for tt in range(3)]
-
-        def slope(tt):
-            at = bank(7 - tt % 2, [P, H], "at%d" % tt)
-            for j in range(4):
-                nc.tensor.transpose(at[:, P * j : P * (j + 1)], a_t[:, j, P * tt : P * (tt + 1)], ident[:])
-            nc.scalar.activation(rt[tt][:], at[:].rearrange("t (p u e) -> t u p e", u=2, e=2), RELU, scale=2.0)
-
-        for tt in range(3):
-            slope(tt)
+        slope(1)
+        slope(2)
 
         st = [bank(tt, [P, H], "st%d" % tt) for tt in range(4)]
         st_last = bank(4, [P, P], "st_last")
@@ -160,7 +166,7 @@ def tile_moe_sub_relu2_kernel(
             for r in range(2):
                 own = "z%d_%d_%d" % (piece, j, r)
                 z = held.tile([P, n], F32, name=own, tag=REUSE.get((piece, j, r), own), align_bytes=64)
-                factor = gate_t[:, r, t0 : t0 + n] if piece == 0 else gl[r][:, j, :]
+                factor = gate_t[r][:, t0 : t0 + n] if piece == 0 else gl[r][:, j, :]
                 nc.vector.tensor_tensor(z[:], y[j][:].indirect(pos_t[r][:, t0 // 16 : (t0 + n) // 16]), factor, MULT)
                 for k in range(n // P):
                     tt = t0 // P + k
@@ -179,21 +185,18 @@ def tile_moe_sub_relu2_kernel(
                 dat[tt][:, :, p0:p1, :], src.rearrange("t (p u e) -> t u p e", u=2, e=2), COPY, scale=2.0
             )
 
-        grouped = {}
+        grouped = [held.tile([P, 4 * n], BF16, name="grouped%d" % t0, align_bytes=64) for t0, n in GROUPS]
 
-        def turn_back(piece, b):
-            t0, n = GROUPS[piece]
-            m = n // P
-            wt = bank(b, [P, m, 2, P], "wt%d" % piece)
-            for k in range(m):
-                words = dat[t0 // P + k][:].rearrange("t u p e -> t (u p e)").bitcast(F32)
-                for u in range(2):
-                    nc.tensor.transpose(wt[:, k, u, :], words[:, P * u : P * (u + 1)], ident[:])
-            g = held.tile([P, 4 * n], BF16, name="grouped%d" % piece, tag="grouped%d" % piece, align_bytes=64)
+        def turn_back(tt, group, b):
+            k = tt - GROUPS[group][0] // P
+            wt = bank(b, [P, 2, P], "wt%d" % tt)
+            words = dat[tt][:].rearrange("t u p e -> t (u p e)").bitcast(F32)
+            for u in range(2):
+                nc.tensor.transpose(wt[:, u, :], words[:, P * u : P * (u + 1)], ident[:])
             nc.scalar.copy(
-                g[:].bitcast(F32).rearrange("p (k t u) -> p k t u", k=m, u=2), wt[:].rearrange("p k u t -> p k t u")
+                grouped[group][:, 4 * P * k : 4 * P * (k + 1)].bitcast(F32).rearrange("p (t u) -> p t u", u=2),
+                wt[:].rearrange("p u t -> p t u"),
             )
-            grouped[piece] = g
 
         def finish(piece, b):
             t0, n = GROUPS[piece]
@@ -220,17 +223,17 @@ def tile_moe_sub_relu2_kernel(
         for tt in range(2):
             new_dat(tt, "dat%d" % tt)
             times_slope(tt, st[tt][:], 0, P)
-        turn_back(0, 5)
+            turn_back(tt, 0, 5 + tt)
         combine(1, 1)
         combine(1, 2)
         new_dat(3, "dat3")
         twice(3, st[3][:, 0 : 3 * P], 0, 96)
-        finish(0, 6)
         combine(1, 3)
         twice(3, st_last[:], 96, P)
         new_dat(2, "gl1")
         times_slope(2, st[2][:], 0, P)
-        turn_back(1, 0)
-        turn_back(2, 1)
+        turn_back(2, 1, 0)
+        turn_back(3, 2, 1)
+        finish(0, 4)
         finish(1, 7)
         finish(2, 5)

@@ -23,7 +23,7 @@ COPY = mybir.ActivationFunctionType.Copy
 
 PIECES = ((0, 384), (384, 128))
 GROUPS = ((0, 256), (256, 128), (384, 128))
-REUSE = {(1, 2, 0): "gate0", (1, 2, 1): "gate1", (1, 3, 0): "rt0", (1, 3, 1): "rt1"}
+REUSE = {(0, 0, 0): "a_last", (1, 2, 0): "gate0", (1, 2, 1): "gate1", (1, 3, 0): "rt0", (1, 3, 1): "rt1"}
 
 
 def tile_moe_sub_relu2_kernel(
@@ -47,7 +47,7 @@ def tile_moe_sub_relu2_kernel(
         w1s = held.tile([P, K], U8, name="w1s", align_bytes=64)
         gate_t = [held.tile([P, T], F32, name="gate%d" % r, tag="gate%d" % r, align_bytes=64) for r in range(2)]
         a_t = held.tile([P, 4, 3 * P], F32, name="a_t")
-        a_last = held.tile([P, 4, P], F32, name="a_last")
+        a_last = held.tile([P, 4, P], F32, name="a_last", tag="a_last", align_bytes=64)
         gl = [held.tile([P, 4, P], F32, name="gl%d" % r, tag="gl%d" % r, align_bytes=64) for r in range(2)]
         ident = held.tile([P, P], F32, name="ident")
         warm = held.tile([P, 8], F32, name="warm")

@@ -21,9 +21,7 @@ MAX = mybir.AluOpType.max
 RELU = mybir.ActivationFunctionType.Relu
 COPY = mybir.ActivationFunctionType.Copy
 
-PIECES = ((0, 384), (384, 128))
 GROUPS = ((0, 256), (256, 128), (384, 128))
-REUSE = {(0, 0, 0): "a_last", (1, 2, 0): "gate0", (1, 2, 1): "gate1", (1, 3, 0): "rt0", (1, 3, 1): "rt1"}
 
 
 def tile_moe_sub_relu2_kernel(
@@ -39,8 +37,8 @@ def tile_moe_sub_relu2_kernel(
 
         offs_t = held.tile([P, S // 16], U16, name="offs_t")
         pos_t = [held.tile([P, T // 16], U16, name="pos_t%d" % r) for r in range(2)]
-        dyw = held.tile([P, T], I32, name="dyw", align_bytes=64)
-        dys = held.tile([P, T], U8, name="dys", align_bytes=64)
+        dyw = held.tile([P, T + 192], I32, name="dyw", align_bytes=64)
+        dys = held.tile([P, 2 * T], U8, name="dys", align_bytes=64)
         w2w = held.tile([P, E, 2 * H], U8, name="w2w", align_bytes=64)
         w2s = held.tile([P, E, H], U8, name="w2s", align_bytes=64)
         w1w = held.tile([P, K], I32, name="w1w", align_bytes=64)
@@ -56,10 +54,12 @@ def tile_moe_sub_relu2_kernel(
         nc.sync.dma_start(offs_t[:], offs)
         for q in range(4):
             (nc.sync if q < 2 else nc.scalar).dma_start(
-                dys[32 * q : 32 * (q + 1), :].bitcast(I32),
+                dys[32 * q : 32 * (q + 1), 0:T].bitcast(I32),
                 dy_scales[0, 4 * q : 4 * q + 4, :].bitcast(I32).unsqueeze(0).to_broadcast([8, 4, T // 4]),
             )
-        nc.scalar.dma_start(dyw[:], dy_words[0].rearrange("p t d -> p (t d)").bitcast(I32))
+        nc.vector.memset(dys[:, T : 2 * T].bitcast(I32), 0)
+        nc.vector.memset(dyw[:, T : T + 192], 0)
+        nc.scalar.dma_start(dyw[:, 0:T], dy_words[0].rearrange("p t d -> p (t d)").bitcast(I32))
         nc.vector.memset(w2s[:].rearrange("p e c -> p (e c)").bitcast(I32), 0)
         nc.gpsimd.memset(warm[:], 0.0)
         nc.gpsimd.memset(w1s[:].bitcast(I32), 0)
@@ -77,125 +77,139 @@ def tile_moe_sub_relu2_kernel(
             nc.sync.dma_start(gate_t[r][:], gate[r])
         nc.sync.dma_start(a_last[:], a_rows[:, :, 3 * P : T])
         nc.sync.dma_start(pos_t[1][:], pos2)
-        nc.sync.dma_start(a_t[:], a_rows[:, :, 0 : 3 * P])
+        nc.sync.dma_start(a_t[:], a.rearrange("(p d) t -> p d t", d=4)[:, :, 0 : 3 * P])
         nc.sync.dma_start(w1w[:], w1t_words[0].rearrange("p k d -> p (k d)").bitcast(I32))
         for q in range(4):
             nc.sync.dma_start(w1s[32 * q : 32 * q + 4, :].bitcast(I32), w1t_scales[0, 4 * q : 4 * q + 4, :].bitcast(I32))
 
-        gw = [held.tile([P, C], U32, name="gw%d" % e, align_bytes=64) for e in range(E)]
-        gs = [held.tile([P, C], U8, name="gs%d" % e, align_bytes=64) for e in range(E)]
+        gw = held.tile([P, S], U32, name="gw", align_bytes=64)
+        gs = held.tile([P, S], U8, name="gs", align_bytes=64)
         y = [held.tile([P, S], F32, name="y%d" % j, tag="y%d" % j, align_bytes=64) for j in range(4)]
 
-        def gather_words(e, c0=0, c1=C):
-            nc.vector.tensor_copy(
-                gw[e][:, c0:c1], dyw[:].bitcast(U32).indirect(offs_t[:, (e * C + c0) // 16 : (e * C + c1) // 16])
-            )
+        def gather_words(s0, s1):
+            nc.vector.tensor_copy(gw[:, s0:s1], dyw[:].bitcast(U32).indirect(offs_t[:, s0 // 16 : s1 // 16]))
 
-        def gather_scales(e):
-            nc.vector.tensor_copy(gs[e][:], dys[:].indirect(offs_t[:, 16 * e : 16 * (e + 1)]))
+        def gather_scales(s0, s1):
+            nc.vector.tensor_copy(gs[:, s0:s1], dys[:].indirect(offs_t[:, s0 // 16 : s1 // 16]))
 
         def expert_mm(acc, e, j, c0=0, c1=C):
             nc.tensor.matmul_mx(
                 out=acc[:, (e % 2) * C + c0 : (e % 2) * C + c1],
                 lhsT=w2w[:, e, 2 * P * j : 2 * P * (j + 1)].bitcast(FP4X4),
                 lhsT_scale=w2s[:, e, P * j : P * (j + 1)],
-                rhs=gw[e][:, c0:c1].bitcast(FP8X4),
-                rhs_scale=gs[e][:, c0:c1],
+                rhs=gw[:, e * C + c0 : e * C + c1].bitcast(FP8X4),
+                rhs_scale=gs[:, e * C + c0 : e * C + c1],
                 start=True,
                 stop=True,
             )
 
-        gather_scales(0)
-        gather_scales(1)
-        gather_words(0)
-        gather_words(1)
-        gather_scales(2)
-        gather_words(2)
-        gather_scales(3)
-        gather_words(3, 0, P)
-        gather_words(3, P, C)
+        gather_scales(0, 2 * C)
+        gather_words(0, 2 * C)
+        gather_scales(2 * C, S)
+        gather_words(2 * C, 3 * C)
+        gather_words(3 * C, 3 * C + P)
+        gather_words(3 * C + P, S)
         for r in range(2):
             nc.vector.scalar_tensor_tensor(
                 gl[r][:], a_last[:], 0.0, gate_t[r][:, 3 * P : T].unsqueeze(1).to_broadcast([P, 4, P]), MAX, MULT
             )
-        rt = [held.tile([P, 2, P, 2], F32, name="rt%d" % tt, tag="rt%d" % tt, align_bytes=64) for tt in range(3)]
-
-        def slope(tt):
-            at = bank((6, 7, 5)[tt], [P, H], "at%d" % tt)
-            for j in range(4):
-                nc.tensor.transpose(at[:, P * j : P * (j + 1)], a_t[:, j, P * tt : P * (tt + 1)], ident[:])
-            nc.scalar.activation(rt[tt][:], at[:].rearrange("t (p u e) -> t u p e", u=2, e=2), RELU, scale=2.0)
-
-        low = [bank(j, [P, 2 * C], "low%d" % j) for j in range(3)]
+        zs = []
+        low = [bank(b, [P, 2 * C], "low%d" % b) for b in (0, 4)]
         expert_mm(low[0], 0, 0)
         expert_mm(low[0], 1, 0)
         nc.scalar.copy(y[0][:, 0 : 2 * C], low[0][:])
-        third = bank(4, [P, 2 * C], "third")
+        expert_mm(low[1], 0, 1)
+        expert_mm(low[1], 1, 1)
+        nc.scalar.copy(y[1][:, 0 : 2 * C], low[1][:])
+        third = bank(1, [P, 2 * C], "third")
         expert_mm(third, 2, 0)
         nc.scalar.copy(y[0][:, 2 * C : 3 * C], third[:, 0:C])
-        expert_mm(low[1], 0, 1)
-        for c0, b in ((0, 5), (P, 3)):
+        for c0, b in ((0, 2), (P, 3)):
             fourth = bank(b, [P, 2 * C], "fourth%d" % c0)
             expert_mm(fourth, 3, 0, c0, c0 + P)
             nc.scalar.copy(y[0][:, 3 * C + c0 : 3 * C + c0 + P], fourth[:, C + c0 : C + c0 + P])
-        low.append(bank(3, [P, 2 * C], "low3"))
-        for j in range(1, 4):
-            if j == 3:
-                slope(0)
-            if j > 1:
-                expert_mm(low[j], 0, j)
-            expert_mm(low[j], 1, j)
-            nc.scalar.copy(y[j][:, 0 : 2 * C], low[j][:])
-            high = bank((6, 7, 4)[j - 1], [P, 2 * C], "high%d" % j)
-            expert_mm(high, 2, j)
-            expert_mm(high, 3, j)
-            nc.scalar.copy(y[j][:, 2 * C : 4 * C], high[:])
+        for j, half, b in ((1, 1, 1), (2, 0, 2), (2, 1, 3), (3, 0, 1), (3, 1, 2)):
+            acc = bank(b, [P, 2 * C], "y%d_%d" % (j, half))
+            expert_mm(acc, 2 * half, j)
+            expert_mm(acc, 2 * half + 1, j)
+            nc.scalar.copy(y[j][:, 2 * C * half : 2 * C * (half + 1)], acc[:])
 
-        slope(1)
-        slope(2)
+        slope = held.tile([P, 3 * P, 4], F32, name="slope", align_bytes=64)
+        dh_t = held.tile([P, 3, 4, P], F32, name="dh_t", align_bytes=64)
 
-        st = [bank(tt, [P, H], "st%d" % tt) for tt in range(4)]
-        st_last = bank(4, [P, P], "st_last")
-        dat = {}
-
-        def new_dat(tt, tag):
-            dat[tt] = held.tile([P, 2, P, 2], BF16, name="dat%d" % tt, tag=tag, align_bytes=64)
-
-        def combine(piece, j):
-            t0, n = PIECES[piece]
+        for j in range(4):
+            if j < 3:
+                whole = bank((0, 4, 3)[j], [P, 3, P], "sums%d" % j)
+                sums = [whole[:, tt, :] for tt in range(3)]
+            else:
+                sums = [bank(5 + tt, [P, P], "sums3_%d" % tt)[:] for tt in range(3)]
             for r in range(2):
-                own = "z%d_%d_%d" % (piece, j, r)
-                z = held.tile([P, n], F32, name=own, tag=REUSE.get((piece, j, r), own), align_bytes=64)
-                factor = gate_t[r][:, t0 : t0 + n] if piece == 0 else gl[r][:, j, :]
-                nc.vector.tensor_tensor(z[:], y[j][:].indirect(pos_t[r][:, t0 // 16 : (t0 + n) // 16]), factor, MULT)
-                for k in range(n // P):
-                    tt = t0 // P + k
-                    dst = st_last[:] if (tt == 3 and j == 3) else st[tt][:, P * j : P * (j + 1)]
-                    nc.tensor.matmul(
-                        dst, z[:, P * k : P * (k + 1)], ident[:], start=(r == 0), stop=(r == 1), is_transpose=True
-                    )
+                own = "z%d_%d" % (j, r)
+                z = held.tile([P, 3 * P], F32, name=own, tag="a_last" if (j, r) == (0, 0) else own, align_bytes=64)
+                nc.vector.tensor_tensor(
+                    z[:], y[j][:].indirect(pos_t[r][:, 0 : 3 * P // 16]), gate_t[r][:, 0 : 3 * P], MULT
+                )
+                zs.append(z)
+            pairs = [(tt, r) for tt in range(3) for r in range(2)]
+            if j == 3:
+                pairs = [(tt, r) for r in range(2) for tt in range(3)]
+            for tt, r in pairs:
+                nc.tensor.matmul(
+                    sums[tt], zs[2 * j + r][:, P * tt : P * (tt + 1)], ident[:],
+                    start=(r == 0), stop=(r == 1), is_transpose=True,
+                )
+            if j == 3:
+                for tt in range(3):
+                    nc.scalar.copy(dh_t[:, tt, :, 96:P], sums[tt].rearrange("t (p d) -> t d p", d=4))
+            else:
+                nc.scalar.copy(dh_t[:, :, :, 32 * j : 32 * (j + 1)], whole[:].rearrange("t k (p d) -> t k d p", d=4))
+                nc.scalar.activation(
+                    slope[:, P * j : P * (j + 1), :],
+                    a_t[:, :, P * j : P * (j + 1)].rearrange("p d t -> p t d"),
+                    RELU,
+                    scale=2.0,
+                )
 
-        def times_slope(tt, src, p0, p1):
-            nc.vector.tensor_tensor(
-                dat[tt][:, :, p0:p1, :], src.rearrange("t (p u e) -> t u p e", u=2, e=2), rt[tt][:, :, p0:p1, :], MULT
-            )
+        back = [bank((0, 4, 1)[tt], [P, 4, P], "back%d" % tt) for tt in range(3)]
+        for tt in range(3):
+            for d in range(4):
+                nc.tensor.transpose(back[tt][:, d, :], dh_t[:, tt, d, :], ident[:])
 
-        def twice(tt, src, p0, p1):
-            nc.scalar.activation(
-                dat[tt][:, :, p0:p1, :], src.rearrange("t (p u e) -> t u p e", u=2, e=2), COPY, scale=2.0
-            )
+        z_last = [held.tile([P, 4, P], F32, name="z_last%d" % r, tag="gate%d" % r, align_bytes=64) for r in range(2)]
+        last_sums = [bank(2, [P, 3 * P], "last_sums0"), bank(3, [P, P], "last_sums1")]
+        da_last = held.tile([P, 2, P, 2], BF16, name="da_last", align_bytes=64)
+        for j in range(4):
+            dst = last_sums[0][:, P * j : P * (j + 1)] if j < 3 else last_sums[1][:]
+            for r in range(2):
+                nc.vector.tensor_tensor(
+                    z_last[r][:, j, :], y[j][:].indirect(pos_t[r][:, 3 * P // 16 : T // 16]), gl[r][:, j, :], MULT
+                )
+                nc.tensor.matmul(dst, z_last[r][:, j, :], ident[:], start=(r == 0), stop=(r == 1), is_transpose=True)
+            if j >= 2:
+                p0, p1 = (0, 96) if j == 2 else (96, P)
+                nc.scalar.activation(
+                    da_last[:, :, p0:p1, :],
+                    last_sums[j - 2][:].rearrange("t (p u e) -> t u p e", u=2, e=2),
+                    COPY,
+                    scale=2.0,
+                )
 
         grouped = [held.tile([P, 4 * n], BF16, name="grouped%d" % t0, align_bytes=64) for t0, n in GROUPS]
+        wt = bank(5, [P, 2, P], "wt")
+        words = da_last[:].rearrange("t u p e -> t (u p e)").bitcast(F32)
+        for u in range(2):
+            nc.tensor.transpose(wt[:, u, :], words[:, P * u : P * (u + 1)], ident[:])
+        nc.scalar.copy(
+            grouped[2][:].bitcast(F32).rearrange("p (t u) -> p t u", u=2), wt[:].rearrange("p u t -> p t u")
+        )
 
-        def turn_back(tt, group, b):
-            k = tt - GROUPS[group][0] // P
-            wt = bank(b, [P, 2, P], "wt%d" % tt)
-            words = dat[tt][:].rearrange("t u p e -> t (u p e)").bitcast(F32)
-            for u in range(2):
-                nc.tensor.transpose(wt[:, u, :], words[:, P * u : P * (u + 1)], ident[:])
-            nc.scalar.copy(
-                grouped[group][:, 4 * P * k : 4 * P * (k + 1)].bitcast(F32).rearrange("p (t u) -> p t u", u=2),
-                wt[:].rearrange("p u t -> p t u"),
+        for tt in range(3):
+            group, k = divmod(tt, 2)
+            nc.vector.tensor_tensor(
+                grouped[group][:, 4 * P * k : 4 * P * (k + 1)].rearrange("p (t d) -> p t d", d=4),
+                back[tt][:].rearrange("p d t -> p t d"),
+                slope[:, P * tt : P * (tt + 1), :],
+                MULT,
             )
 
         def finish(piece, b):
@@ -217,23 +231,6 @@ def tile_moe_sub_relu2_kernel(
             nc.scalar.copy(res[:], acc[:])
             nc.sync.dma_start(out[:, t0 : t0 + n], res[:])
 
-        for j in range(4):
-            combine(0, j)
-        combine(1, 0)
-        for tt in range(2):
-            new_dat(tt, "dat%d" % tt)
-            times_slope(tt, st[tt][:], 0, P)
-            turn_back(tt, 0, 5 + tt)
-        combine(1, 1)
-        combine(1, 2)
-        new_dat(3, "dat3")
-        twice(3, st[3][:, 0 : 3 * P], 0, 96)
-        combine(1, 3)
-        twice(3, st_last[:], 96, P)
-        new_dat(2, "gl1")
-        times_slope(2, st[2][:], 0, P)
-        turn_back(2, 1, 0)
-        turn_back(3, 2, 1)
-        finish(0, 4)
+        finish(0, 6)
         finish(1, 7)
-        finish(2, 5)
+        finish(2, 2)

@@ -48,8 +48,6 @@ def tile_moe_sub_relu2_kernel(
         a_last = held.tile([P, 4, P], F32, name="a_last", tag="a_last", align_bytes=64)
         gl = [held.tile([P, 4, P], F32, name="gl%d" % r, tag="gl%d" % r, align_bytes=64) for r in range(2)]
         ident = held.tile([P, P], F32, name="ident")
-        warm = held.tile([P, 8], F32, name="warm")
-        warm2 = held.tile([P, 8], F32, name="warm2")
 
         nc.sync.dma_start(offs_t[:], offs)
         for q in range(4):
@@ -61,9 +59,7 @@ def tile_moe_sub_relu2_kernel(
         nc.vector.memset(dyw[:, T : T + 192], 0)
         nc.scalar.dma_start(dyw[:, 0:T], dy_words[0].rearrange("p t d -> p (t d)").bitcast(I32))
         nc.vector.memset(w2s[:].rearrange("p e c -> p (e c)").bitcast(I32), 0)
-        nc.gpsimd.memset(warm[:], 0.0)
         nc.gpsimd.memset(w1s[:].bitcast(I32), 0)
-        nc.scalar.activation(warm2[:], warm[:], RELU)
         make_identity(nc, ident[:])
         a_rows = a.rearrange("(j p) t -> p j t", p=P)
         nc.sync.dma_start(pos_t[0][:], pos1)
@@ -134,7 +130,6 @@ def tile_moe_sub_relu2_kernel(
             expert_mm(acc, 2 * half + 1, j)
             nc.scalar.copy(y[j][:, 2 * C * half : 2 * C * (half + 1)], acc[:])
 
-        slope = held.tile([P, 3 * P, 4], F32, name="slope", align_bytes=64)
         dh_t = held.tile([P, 3, 4, P], F32, name="dh_t", align_bytes=64)
 
         for j in range(4):
@@ -160,15 +155,24 @@ def tile_moe_sub_relu2_kernel(
                 )
             if j == 3:
                 for tt in range(3):
-                    nc.scalar.copy(dh_t[:, tt, :, 96:P], sums[tt].rearrange("t (p d) -> t d p", d=4))
+                    nc.scalar.copy(
+                        dh_t[:, tt, :, 96:P].rearrange("t d p -> t p d"), sums[tt].rearrange("t (p d) -> t p d", d=4)
+                    )
             else:
-                nc.scalar.copy(dh_t[:, :, :, 32 * j : 32 * (j + 1)], whole[:].rearrange("t k (p d) -> t k d p", d=4))
-                nc.scalar.activation(
-                    slope[:, P * j : P * (j + 1), :],
-                    a_t[:, :, P * j : P * (j + 1)].rearrange("p d t -> p t d"),
-                    RELU,
-                    scale=2.0,
+                nc.scalar.copy(
+                    dh_t[:, :, :, 32 * j : 32 * (j + 1)].rearrange("t k d p -> t k p d"),
+                    whole[:].rearrange("t k (p d) -> t k p d", d=4),
                 )
+
+        slope = []
+        for tt, tag in enumerate(("slope0", "z3_0", "z3_1")):
+            slope.append(held.tile([P, P, 4], F32, name="slope%d" % tt, tag=tag, align_bytes=64))
+            nc.scalar.activation(
+                slope[tt][:].rearrange("p (c i) d -> p c d i", i=4),
+                a_t[:, :, P * tt : P * (tt + 1)].rearrange("p d (c i) -> p c d i", i=4),
+                RELU,
+                scale=2.0,
+            )
 
         back = [bank((0, 4, 1)[tt], [P, 4, P], "back%d" % tt) for tt in range(3)]
         for tt in range(3):
@@ -208,7 +212,7 @@ def tile_moe_sub_relu2_kernel(
             nc.vector.tensor_tensor(
                 grouped[group][:, 4 * P * k : 4 * P * (k + 1)].rearrange("p (t d) -> p t d", d=4),
                 back[tt][:].rearrange("p d t -> p t d"),
-                slope[:, P * tt : P * (tt + 1), :],
+                slope[tt][:],
                 MULT,
             )
 
@@ -231,6 +235,6 @@ def tile_moe_sub_relu2_kernel(
             nc.scalar.copy(res[:], acc[:])
             nc.sync.dma_start(out[:, t0 : t0 + n], res[:])
 
-        finish(0, 6)
-        finish(1, 7)
+        finish(0, 3)
+        finish(1, 5)
         finish(2, 2)

@@ -175,31 +175,39 @@ def tile_moe_sub_relu2_kernel(
             )
 
         back = [bank((0, 4, 1)[tt], [P, 4, P], "back%d" % tt) for tt in range(3)]
-        for tt in range(3):
+        z_last = [held.tile([P, 4, P], F32, name="z_last%d" % r, tag="gate%d" % r, align_bytes=64) for r in range(2)]
+        last_sums = [bank(2, [P, P], "last_sums0"), bank(5, [P, 2 * P], "last_sums1"), bank(6, [P, P], "last_sums2")]
+        da_last = held.tile([P, 2, P, 2], BF16, name="da_last", align_bytes=64)
+
+        def turn_back(tt):
             for d in range(4):
                 nc.tensor.transpose(back[tt][:, d, :], dh_t[:, tt, d, :], ident[:])
 
-        z_last = [held.tile([P, 4, P], F32, name="z_last%d" % r, tag="gate%d" % r, align_bytes=64) for r in range(2)]
-        last_sums = [bank(2, [P, 3 * P], "last_sums0"), bank(3, [P, P], "last_sums1")]
-        da_last = held.tile([P, 2, P, 2], BF16, name="da_last", align_bytes=64)
-        for j in range(4):
-            dst = last_sums[0][:, P * j : P * (j + 1)] if j < 3 else last_sums[1][:]
+        def last_tokens(j, dst):
             for r in range(2):
                 nc.vector.tensor_tensor(
                     z_last[r][:, j, :], y[j][:].indirect(pos_t[r][:, 3 * P // 16 : T // 16]), gl[r][:, j, :], MULT
                 )
                 nc.tensor.matmul(dst, z_last[r][:, j, :], ident[:], start=(r == 0), stop=(r == 1), is_transpose=True)
-            if j >= 2:
-                p0, p1 = (0, 96) if j == 2 else (96, P)
-                nc.scalar.activation(
-                    da_last[:, :, p0:p1, :],
-                    last_sums[j - 2][:].rearrange("t (p u e) -> t u p e", u=2, e=2),
-                    COPY,
-                    scale=2.0,
-                )
+
+        def round_last(part, p0, p1):
+            nc.scalar.activation(
+                da_last[:, :, p0:p1, :], last_sums[part][:].rearrange("t (p u e) -> t u p e", u=2, e=2), COPY, scale=2.0
+            )
+
+        last_tokens(0, last_sums[0][:])
+        turn_back(0)
+        last_tokens(1, last_sums[1][:, 0:P])
+        turn_back(1)
+        round_last(0, 0, 32)
+        last_tokens(2, last_sums[1][:, P : 2 * P])
+        round_last(1, 32, 96)
+        last_tokens(3, last_sums[2][:])
+        round_last(2, 96, P)
+        turn_back(2)
 
         grouped = [held.tile([P, 4 * n], BF16, name="grouped%d" % t0, align_bytes=64) for t0, n in GROUPS]
-        wt = bank(5, [P, 2, P], "wt")
+        wt = bank(7, [P, 2, P], "wt")
         words = da_last[:].rearrange("t u p e -> t (u p e)").bitcast(F32)
         for u in range(2):
             nc.tensor.transpose(wt[:, u, :], words[:, P * u : P * (u + 1)], ident[:])
@@ -235,6 +243,6 @@ def tile_moe_sub_relu2_kernel(
             nc.scalar.copy(res[:], acc[:])
             nc.sync.dma_start(out[:, t0 : t0 + n], res[:])
 
-        finish(0, 3)
-        finish(1, 5)
+        finish(0, 6)
+        finish(1, 7)
         finish(2, 2)

@@ -43,7 +43,7 @@ def tile_moe_sub_relu2_kernel(
         w2s = held.tile([P, E, H], U8, name="w2s", align_bytes=64)
         w1w = held.tile([P, K], I32, name="w1w", align_bytes=64)
         w1s = held.tile([P, K], U8, name="w1s", align_bytes=64)
-        gate_t = [held.tile([P, T], F32, name="gate%d" % r, tag="gate%d" % r, align_bytes=64) for r in range(2)]
+        gate_t = [held.tile([P, T + 2 * P * (1 - r)], F32, name="gate%d" % r, tag="gate%d" % r, align_bytes=64) for r in range(2)]
         a_t = held.tile([P, 4, 3 * P], F32, name="a_t")
         a_last = held.tile([P, 4, P], F32, name="a_last", tag="a_last", align_bytes=64)
         gl = [held.tile([P, 4, P], F32, name="gl%d" % r, tag="gl%d" % r, align_bytes=64) for r in range(2)]
@@ -70,7 +70,7 @@ def tile_moe_sub_relu2_kernel(
                 w2t_scales[:, 0, 4 * q : 4 * q + 4, :].rearrange("e r c -> r e c").bitcast(I32),
             )
         for r in range(2):
-            nc.sync.dma_start(gate_t[r][:], gate[r])
+            nc.sync.dma_start(gate_t[r][:, 0:T], gate[r])
         nc.sync.dma_start(a_last[:], a_rows[:, :, 3 * P : T])
         nc.sync.dma_start(pos_t[1][:], pos2)
         nc.sync.dma_start(a_t[:], a.rearrange("(p d) t -> p d t", d=4)[:, :, 0 : 3 * P])
@@ -140,9 +140,12 @@ def tile_moe_sub_relu2_kernel(
                 sums = [bank(5 + tt, [P, P], "sums3_%d" % tt)[:] for tt in range(3)]
             for r in range(2):
                 own = "z%d_%d" % (j, r)
-                z = held.tile([P, 3 * P], F32, name=own, tag="a_last" if (j, r) == (0, 0) else own, align_bytes=64)
+                if (j, r) == (0, 0):
+                    z = gate_t[0][:, 3 * P : 6 * P]
+                else:
+                    z = held.tile([P, 3 * P], F32, name=own, tag=own, align_bytes=64)[:]
                 nc.vector.tensor_tensor(
-                    z[:], y[j][:].indirect(pos_t[r][:, 0 : 3 * P // 16]), gate_t[r][:, 0 : 3 * P], MULT
+                    z, y[j][:].indirect(pos_t[r][:, 0 : 3 * P // 16]), gate_t[r][:, 0 : 3 * P], MULT
                 )
                 zs.append(z)
             pairs = [(tt, r) for tt in range(3) for r in range(2)]

@@ -18,10 +18,9 @@ FP8X4 = mybir.dt.float8_e4m3fn_x4
 FP4X4 = mybir.dt.float4_e2m1fn_x4
 MULT = mybir.AluOpType.mult
 MAX = mybir.AluOpType.max
-RELU = mybir.ActivationFunctionType.Relu
+ADD = mybir.AluOpType.add
 COPY = mybir.ActivationFunctionType.Copy
-
-GROUPS = ((0, 256), (256, 128), (384, 128))
+RELU = mybir.ActivationFunctionType.Relu
 
 
 def tile_moe_sub_relu2_kernel(
@@ -39,14 +38,15 @@ def tile_moe_sub_relu2_kernel(
         pos_t = [held.tile([P, T // 16], U16, name="pos_t%d" % r) for r in range(2)]
         dyw = held.tile([P, T + 192], I32, name="dyw", align_bytes=64)
         dys = held.tile([P, 2 * T], U8, name="dys", align_bytes=64)
-        w2w = held.tile([P, E, 2 * H], U8, name="w2w", align_bytes=64)
-        w2s = held.tile([P, E, H], U8, name="w2s", align_bytes=64)
+        w2w = held.tile([P, E, 2 * H], U8, name="w2w", tag="w2w", align_bytes=64)
+        w2s = held.tile([P, E, H], U8, name="w2s", tag="w2s", align_bytes=64)
         w1w = held.tile([P, K], I32, name="w1w", align_bytes=64)
         w1s = held.tile([P, K], U8, name="w1s", align_bytes=64)
-        gate_t = [held.tile([P, T + 2 * P * (1 - r)], F32, name="gate%d" % r, tag="gate%d" % r, align_bytes=64) for r in range(2)]
+        gate_t = [held.tile([P, 4 * P], F32, name="gate%d" % r, tag="gate%d" % r, align_bytes=64) for r in range(2)]
+        gate_col = held.tile([P, 2], F32, name="gate_col", tag="gate_col", align_bytes=64)
         a_t = held.tile([P, 4, 3 * P], F32, name="a_t")
-        a_last = held.tile([P, 4, P], F32, name="a_last", tag="a_last", align_bytes=64)
-        gl = [held.tile([P, 4, P], F32, name="gl%d" % r, tag="gl%d" % r, align_bytes=64) for r in range(2)]
+        a_last = held.tile([P, 4, P], F32, name="a_last", align_bytes=64)
+        gl = [held.tile([P, 4, P], F32, name="gl%d" % r, align_bytes=64) for r in range(2)]
         ident = held.tile([P, P], F32, name="ident")
 
         nc.sync.dma_start(offs_t[:], offs)
@@ -61,7 +61,6 @@ def tile_moe_sub_relu2_kernel(
         nc.vector.memset(w2s[:].rearrange("p e c -> p (e c)").bitcast(I32), 0)
         nc.gpsimd.memset(w1s[:].bitcast(I32), 0)
         make_identity(nc, ident[:])
-        a_rows = a.rearrange("(j p) t -> p j t", p=P)
         nc.sync.dma_start(pos_t[0][:], pos1)
         nc.sync.dma_start(w2w[:].bitcast(I32), w2t_words[:, 0].rearrange("e p c -> p e c").bitcast(I32))
         for q in range(4):
@@ -70,17 +69,19 @@ def tile_moe_sub_relu2_kernel(
                 w2t_scales[:, 0, 4 * q : 4 * q + 4, :].rearrange("e r c -> r e c").bitcast(I32),
             )
         for r in range(2):
-            nc.sync.dma_start(gate_t[r][:, 0:T], gate[r])
-        nc.sync.dma_start(a_last[:], a_rows[:, :, 3 * P : T])
+            nc.sync.dma_start(gate_t[r][:, 0 : 3 * P], gate[r][:, P:T])
+        nc.sync.dma_start(a_last[:], a.rearrange("(j p) t -> p j t", p=P)[:, :, 3 * P : T])
         nc.sync.dma_start(pos_t[1][:], pos2)
-        nc.sync.dma_start(a_t[:], a.rearrange("(p d) t -> p d t", d=4)[:, :, 0 : 3 * P])
+        with nc.allow_non_contiguous_dma(reason="one gate a partition"):
+            nc.sync.dma_start(gate_col[:], gate[:, 0, 0:P].rearrange("r t -> t r"))
         nc.sync.dma_start(w1w[:], w1t_words[0].rearrange("p k d -> p (k d)").bitcast(I32))
         for q in range(4):
             nc.sync.dma_start(w1s[32 * q : 32 * q + 4, :].bitcast(I32), w1t_scales[0, 4 * q : 4 * q + 4, :].bitcast(I32))
+        nc.sync.dma_start(a_t[:], a.rearrange("(p d) t -> p d t", d=4)[:, :, 0 : 3 * P])
 
         gw = held.tile([P, S], U32, name="gw", align_bytes=64)
         gs = held.tile([P, S], U8, name="gs", align_bytes=64)
-        y = [held.tile([P, S], F32, name="y%d" % j, tag="y%d" % j, align_bytes=64) for j in range(4)]
+        y = [held.tile([P, S], F32, name="y%d" % j, align_bytes=64) for j in range(4)]
 
         def gather_words(s0, s1):
             nc.vector.tensor_copy(gw[:, s0:s1], dyw[:].bitcast(U32).indirect(offs_t[:, s0 // 16 : s1 // 16]))
@@ -88,16 +89,21 @@ def tile_moe_sub_relu2_kernel(
         def gather_scales(s0, s1):
             nc.vector.tensor_copy(gs[:, s0:s1], dys[:].indirect(offs_t[:, s0 // 16 : s1 // 16]))
 
-        def expert_mm(acc, e, j, c0=0, c1=C):
-            nc.tensor.matmul_mx(
-                out=acc[:, (e % 2) * C + c0 : (e % 2) * C + c1],
-                lhsT=w2w[:, e, 2 * P * j : 2 * P * (j + 1)].bitcast(FP4X4),
-                lhsT_scale=w2s[:, e, P * j : P * (j + 1)],
-                rhs=gw[:, e * C + c0 : e * C + c1].bitcast(FP8X4),
-                rhs_scale=gs[:, e * C + c0 : e * C + c1],
-                start=True,
-                stop=True,
-            )
+        def products(j, s0, s1, b):
+            acc = bank(b, [P, s1 - s0], "y%d_%d" % (j, s0))
+            for c0 in range(s0, s1, C):
+                c1 = min(c0 + C, s1)
+                e = c0 // C
+                nc.tensor.matmul_mx(
+                    out=acc[:, c0 - s0 : c1 - s0],
+                    lhsT=w2w[:, e, 2 * P * j : 2 * P * (j + 1)].bitcast(FP4X4),
+                    lhsT_scale=w2s[:, e, P * j : P * (j + 1)],
+                    rhs=gw[:, c0:c1].bitcast(FP8X4),
+                    rhs_scale=gs[:, c0:c1],
+                    start=True,
+                    stop=True,
+                )
+            nc.scalar.copy(y[j][:, s0:s1], acc[:])
 
         gather_scales(0, 2 * C)
         gather_words(0, 2 * C)
@@ -107,131 +113,184 @@ def tile_moe_sub_relu2_kernel(
         gather_words(3 * C + P, S)
         for r in range(2):
             nc.vector.scalar_tensor_tensor(
-                gl[r][:], a_last[:], 0.0, gate_t[r][:, 3 * P : T].unsqueeze(1).to_broadcast([P, 4, P]), MAX, MULT
+                gl[r][:], a_last[:], 0.0, gate_t[r][:, 2 * P : 3 * P].unsqueeze(1).to_broadcast([P, 4, P]), MAX, MULT
             )
-        zs = []
-        low = [bank(b, [P, 2 * C], "low%d" % b) for b in (0, 4)]
-        expert_mm(low[0], 0, 0)
-        expert_mm(low[0], 1, 0)
-        nc.scalar.copy(y[0][:, 0 : 2 * C], low[0][:])
-        expert_mm(low[1], 0, 1)
-        expert_mm(low[1], 1, 1)
-        nc.scalar.copy(y[1][:, 0 : 2 * C], low[1][:])
-        third = bank(1, [P, 2 * C], "third")
-        expert_mm(third, 2, 0)
-        nc.scalar.copy(y[0][:, 2 * C : 3 * C], third[:, 0:C])
-        for c0, b in ((0, 2), (P, 3)):
-            fourth = bank(b, [P, 2 * C], "fourth%d" % c0)
-            expert_mm(fourth, 3, 0, c0, c0 + P)
-            nc.scalar.copy(y[0][:, 3 * C + c0 : 3 * C + c0 + P], fourth[:, C + c0 : C + c0 + P])
-        for j, half, b in ((1, 1, 1), (2, 0, 2), (2, 1, 3), (3, 0, 1), (3, 1, 2)):
-            acc = bank(b, [P, 2 * C], "y%d_%d" % (j, half))
-            expert_mm(acc, 2 * half, j)
-            expert_mm(acc, 2 * half + 1, j)
-            nc.scalar.copy(y[j][:, 2 * C * half : 2 * C * (half + 1)], acc[:])
 
-        dh_t = held.tile([P, 3, 4, P], F32, name="dh_t", align_bytes=64)
+        products(0, 0, 2 * C, 0)
+        products(1, 0, 2 * C, 4)
+        products(2, 0, 2 * C, 6)
+        products(0, 2 * C, 3 * C, 1)
+        products(0, 3 * C, 3 * C + P, 2)
+        products(0, 3 * C + P, S, 3)
+        products(1, 2 * C, S, 5)
+        products(2, 2 * C, S, 7)
+        products(3, 0, 2 * C, 0)
+        products(3, 2 * C, S, 4)
 
-        for j in range(4):
-            if j < 3:
-                whole = bank((0, 4, 3)[j], [P, 3, P], "sums%d" % j)
-                sums = [whole[:, tt, :] for tt in range(3)]
+        def picked(j, r, t0, t1):
+            return y[j][:].indirect(pos_t[r][:, t0 // 16 : t1 // 16])
+
+        def turn(dst, src, start, stop):
+            nc.tensor.matmul(dst, src, ident[:], start=start, stop=stop, is_transpose=True)
+
+        dh_t = held.tile([P, 2, 4, P], F32, name="dh_t", align_bytes=64)
+
+        def main_tokens(j, banks):
+            if len(banks) == 1:
+                whole = bank(banks[0], [P, 2, P], "sums%d" % j)
+                sums = [whole[:, k, :] for k in range(2)]
             else:
-                sums = [bank(5 + tt, [P, P], "sums3_%d" % tt)[:] for tt in range(3)]
+                sums = [bank(b, [P, P], "sums%d_%d" % (j, b))[:] for b in banks]
+            z = []
             for r in range(2):
-                own = "z%d_%d" % (j, r)
                 if (j, r) == (0, 0):
-                    z = gate_t[0][:, 3 * P : 6 * P]
+                    z.append(gate_t[0][:, 2 * P : 4 * P])
                 else:
-                    z = held.tile([P, 3 * P], F32, name=own, tag=own, align_bytes=64)[:]
-                nc.vector.tensor_tensor(
-                    z, y[j][:].indirect(pos_t[r][:, 0 : 3 * P // 16]), gate_t[r][:, 0 : 3 * P], MULT
-                )
-                zs.append(z)
-            pairs = [(tt, r) for tt in range(3) for r in range(2)]
-            if j == 3:
-                pairs = [(tt, r) for r in range(2) for tt in range(3)]
-            for tt, r in pairs:
-                nc.tensor.matmul(
-                    sums[tt], zs[2 * j + r][:, P * tt : P * (tt + 1)], ident[:],
-                    start=(r == 0), stop=(r == 1), is_transpose=True,
-                )
-            if j == 3:
-                for tt in range(3):
-                    nc.scalar.copy(
-                        dh_t[:, tt, :, 96:P].rearrange("t d p -> t p d"), sums[tt].rearrange("t (p d) -> t p d", d=4)
-                    )
-            else:
+                    z.append(held.tile([P, 2 * P], F32, name="z%d_%d" % (j, r), align_bytes=64)[:])
+                nc.vector.tensor_tensor(z[r], picked(j, r, P, 3 * P), gate_t[r][:, 0 : 2 * P], MULT)
+            if len(banks) == 1:
+                for k in range(2):
+                    for r in range(2):
+                        turn(sums[k], z[r][:, P * k : P * (k + 1)], r == 0, r == 1)
                 nc.scalar.copy(
                     dh_t[:, :, :, 32 * j : 32 * (j + 1)].rearrange("t k d p -> t k p d"),
                     whole[:].rearrange("t k (p d) -> t k p d", d=4),
                 )
+            else:
+                for r in range(2):
+                    for k in range(2):
+                        turn(sums[k], z[r][:, P * k : P * (k + 1)], r == 0, r == 1)
+                for k in range(2):
+                    nc.scalar.copy(
+                        dh_t[:, k, :, 32 * j : 32 * (j + 1)].rearrange("t d p -> t p d"),
+                        sums[k].rearrange("t (p d) -> t p d", d=4),
+                    )
 
-        slope = []
-        for tt, tag in enumerate(("slope0", "z3_0", "z3_1")):
-            slope.append(held.tile([P, P, 4], F32, name="slope%d" % tt, tag=tag, align_bytes=64))
+        raw = [held.tile([P, 4, P], F32, name="raw%d" % r, tag=("w2s", "w2w")[r], align_bytes=64) for r in range(2)]
+        gated = held.tile([P, 4, P], F32, name="gated", tag="gated", align_bytes=64)
+        dh_first = held.tile([P, 4, P], F32, name="dh_first", align_bytes=64)
+        turned = {}
+
+        def first_tokens(r, j, b, width):
+            if b not in turned:
+                turned[b] = bank(b, [P, width, P], "turned%d" % b)
+            nc.scalar.activation(raw[r][:, j, :], picked(j, r, 0, P), COPY)
+            turn(turned[b][:, j % width, :], raw[r][:, j, :], True, True)
+
+        def times_gate(half, b):
             nc.scalar.activation(
-                slope[tt][:].rearrange("p (c i) d -> p c d i", i=4),
-                a_t[:, :, P * tt : P * (tt + 1)].rearrange("p d (c i) -> p c d i", i=4),
-                RELU,
-                scale=2.0,
+                gated[:, :, 64 * half : 64 * (half + 1)],
+                turned[b][:].rearrange("t j (q d) -> t d (j q)", d=4),
+                COPY,
+                scale=gate_col[:, 0:1],
             )
 
-        back = [bank((0, 4, 1)[tt], [P, 4, P], "back%d" % tt) for tt in range(3)]
-        z_last = [held.tile([P, 4, P], F32, name="z_last%d" % r, tag="gate%d" % r, align_bytes=64) for r in range(2)]
-        last_sums = [bank(2, [P, P], "last_sums0"), bank(5, [P, 2 * P], "last_sums1"), bank(6, [P, P], "last_sums2")]
-        da_last = held.tile([P, 2, P, 2], BF16, name="da_last", align_bytes=64)
+        def sum_first():
+            nc.vector.scalar_tensor_tensor(
+                dh_first[:],
+                turned[0][:].rearrange("t j (q d) -> t d (j q)", d=4),
+                gate_col[:, 1:2],
+                gated[:],
+                MULT,
+                ADD,
+            )
 
-        def turn_back(tt):
+        main_tokens(0, (1,))
+        main_tokens(1, (2,))
+        first_tokens(0, 0, 7, 2)
+        first_tokens(0, 1, 7, 2)
+        main_tokens(2, (3,))
+        first_tokens(0, 2, 2, 2)
+        first_tokens(0, 3, 2, 2)
+        main_tokens(3, (5, 6))
+
+        back = [bank(b, [P, 4, P], "back%d" % tt) for tt, b in enumerate((4, 1))]
+        z_last = [held.tile([P, 4, P], F32, name="z_last%d" % r, tag="gate%d" % r, align_bytes=64) for r in range(2)]
+        last_sums = [bank(6, [P, 2 * P], "last_sums0")]
+
+        def turn_back(k):
             for d in range(4):
-                nc.tensor.transpose(back[tt][:, d, :], dh_t[:, tt, d, :], ident[:])
+                turn(back[1 + k][:, d, :], dh_t[:, k, d, :], True, True)
+
+        def turn_back_first():
+            for d in range(4):
+                turn(back[0][:, d, :], dh_first[:, d, :], True, True)
 
         def last_tokens(j, dst):
             for r in range(2):
-                nc.vector.tensor_tensor(
-                    z_last[r][:, j, :], y[j][:].indirect(pos_t[r][:, 3 * P // 16 : T // 16]), gl[r][:, j, :], MULT
-                )
-                nc.tensor.matmul(dst, z_last[r][:, j, :], ident[:], start=(r == 0), stop=(r == 1), is_transpose=True)
+                nc.vector.tensor_tensor(z_last[r][:, j, :], picked(j, r, 3 * P, T), gl[r][:, j, :], MULT)
+                turn(dst, z_last[r][:, j, :], r == 0, r == 1)
 
         def round_last(part, p0, p1):
-            nc.scalar.activation(
-                da_last[:, :, p0:p1, :], last_sums[part][:].rearrange("t (p u e) -> t u p e", u=2, e=2), COPY, scale=2.0
-            )
+            nc.scalar.copy(da_last[:, :, p0:p1, :], last_sums[part][:].rearrange("t (p u e) -> t u p e", u=2, e=2))
 
-        last_tokens(0, last_sums[0][:])
+        da_last = held.tile([P, 2, P, 2], BF16, name="da_last", align_bytes=64)
         turn_back(0)
-        last_tokens(1, last_sums[1][:, 0:P])
-        turn_back(1)
-        round_last(0, 0, 32)
-        last_tokens(2, last_sums[1][:, P : 2 * P])
-        round_last(1, 32, 96)
+        last_tokens(0, last_sums[0][:, 0:P])
+        first_tokens(1, 0, 0, 4)
+        last_tokens(1, last_sums[0][:, P : 2 * P])
+        times_gate(0, 7)
+        first_tokens(1, 1, 0, 4)
+        last_sums.append(bank(7, [P, P], "last_sums1"))
+        last_tokens(2, last_sums[1][:])
+        first_tokens(1, 2, 0, 4)
+        first_tokens(1, 3, 0, 4)
+        times_gate(1, 2)
+        last_sums.append(bank(2, [P, P], "last_sums2"))
         last_tokens(3, last_sums[2][:])
+        slope_middle = held.tile([P, 2 * P, 4], F32, name="slope_middle", align_bytes=64)
+        nc.vector.tensor_scalar_max(
+            slope_middle[:].rearrange("p (c i) d -> p c d i", i=4),
+            a_t[:, :, P : 3 * P].rearrange("p d (c i) -> p c d i", i=4),
+            0.0,
+        )
+        round_last(0, 0, 64)
+        back.append(bank(6, [P, 4, P], "back2"))
+        turn_back(1)
+        round_last(1, 64, 96)
         round_last(2, 96, P)
-        turn_back(2)
+        slope_first = held.tile([P, P, 4], F32, name="slope_first", tag="w2w", align_bytes=64)
+        nc.scalar.activation(
+            slope_first[:].rearrange("p (c i) d -> p c d i", i=4),
+            a_t[:, :, 0:P].rearrange("p d (c i) -> p c d i", i=4),
+            RELU,
+        )
+        slope = [slope_first[:], slope_middle[:, 0:P, :], slope_middle[:, P : 2 * P, :]]
+        sum_first()
+        turn_back_first()
 
-        grouped = [held.tile([P, 4 * n], BF16, name="grouped%d" % t0, align_bytes=64) for t0, n in GROUPS]
-        wt = bank(7, [P, 2, P], "wt")
+        groups = ((0, P), (P, 2 * P), (3 * P, P))
+        middle = held.tile([P, 2, 4 * P], BF16, name="middle", tag="gated", align_bytes=64)
+        grouped = [
+            held.tile([P, 4 * P], BF16, name="grouped0", align_bytes=64)[:],
+            middle[:, 0, :],
+            middle[:, 1, :],
+            held.tile([P, 4 * P], BF16, name="grouped3", align_bytes=64)[:],
+        ]
+        wt = bank(3, [P, 2, P], "wt")
         words = da_last[:].rearrange("t u p e -> t (u p e)").bitcast(F32)
         for u in range(2):
-            nc.tensor.transpose(wt[:, u, :], words[:, P * u : P * (u + 1)], ident[:])
+            turn(wt[:, u, :], words[:, P * u : P * (u + 1)], True, True)
         nc.scalar.copy(
-            grouped[2][:].bitcast(F32).rearrange("p (t u) -> p t u", u=2), wt[:].rearrange("p u t -> p t u")
+            grouped[3][:].bitcast(F32).rearrange("p (t u) -> p t u", u=2), wt[:].rearrange("p u t -> p t u")
         )
 
-        for tt in range(3):
-            group, k = divmod(tt, 2)
+        def times_slope(tt):
             nc.vector.tensor_tensor(
-                grouped[group][:, 4 * P * k : 4 * P * (k + 1)].rearrange("p (t d) -> p t d", d=4),
+                grouped[tt][:].rearrange("p (t d) -> p t d", d=4),
                 back[tt][:].rearrange("p d t -> p t d"),
-                slope[tt][:],
+                slope[tt],
                 MULT,
             )
 
         def finish(piece, b):
-            t0, n = GROUPS[piece]
+            t0, n = groups[piece]
             codes = held.tile([P, n], U32, name="codes%d" % piece, align_bytes=64)
             scales = held.tile([P, n], U8, name="scales%d" % piece, align_bytes=64)
-            nc.vector.quantize_mx(out=codes[:].bitcast(FP8X4), scales=scales[:], in_=grouped[piece][:])
+            for c0 in range(0, n, P):
+                nc.vector.quantize_mx(
+                    out=codes[:, c0 : c0 + P].bitcast(FP8X4), scales=scales[:, c0 : c0 + P], in_=grouped[(t0 + c0) // P][:]
+                )
             acc = bank(b, [P, n], "acc_out%d" % piece)
             nc.tensor.matmul_mx(
                 out=acc[:],
@@ -243,9 +302,12 @@ def tile_moe_sub_relu2_kernel(
                 stop=True,
             )
             res = held.tile([P, n], F32, name="res%d" % piece)
-            nc.scalar.copy(res[:], acc[:])
+            nc.scalar.activation(res[:], acc[:], COPY, scale=2.0)
             nc.sync.dma_start(out[:, t0 : t0 + n], res[:])
 
-        finish(0, 6)
-        finish(1, 7)
-        finish(2, 2)
+        times_slope(1)
+        times_slope(2)
+        finish(1, 0)
+        times_slope(0)
+        finish(2, 5)
+        finish(0, 1)

@@ -42,8 +42,8 @@ def tile_moe_sub_relu2_kernel(
         w2s = held.tile([P, E, H], U8, name="w2s", tag="w2s", align_bytes=64)
         w1w = held.tile([P, K], I32, name="w1w", align_bytes=64)
         w1s = held.tile([P, K], U8, name="w1s", align_bytes=64)
-        gate_t = [held.tile([P, 4 * P], F32, name="gate%d" % r, tag="gate%d" % r, align_bytes=64) for r in range(2)]
-        gate_col = held.tile([P, 2], F32, name="gate_col", tag="gate_col", align_bytes=64)
+        gate_t = [held.tile([P, 6 * P], F32, name="gate%d" % r, tag="gate%d" % r, align_bytes=64) for r in range(2)]
+        gate_col = held.tile([P, 2], F32, name="gate_col")
         a_t = held.tile([P, 4, 3 * P], F32, name="a_t")
         a_last = held.tile([P, 4, P], F32, name="a_last", align_bytes=64)
         gl = [held.tile([P, 4, P], F32, name="gl%d" % r, align_bytes=64) for r in range(2)]
@@ -69,15 +69,15 @@ def tile_moe_sub_relu2_kernel(
                 w2t_scales[:, 0, 4 * q : 4 * q + 4, :].rearrange("e r c -> r e c").bitcast(I32),
             )
         for r in range(2):
-            nc.sync.dma_start(gate_t[r][:, 0 : 3 * P], gate[r][:, P:T])
+            nc.sync.dma_start(gate_t[r][:, 0:T], gate[r])
         nc.sync.dma_start(a_last[:], a.rearrange("(j p) t -> p j t", p=P)[:, :, 3 * P : T])
         nc.sync.dma_start(pos_t[1][:], pos2)
         with nc.allow_non_contiguous_dma(reason="one gate a partition"):
             nc.sync.dma_start(gate_col[:], gate[:, 0, 0:P].rearrange("r t -> t r"))
+        nc.sync.dma_start(a_t[:], a.rearrange("(p d) t -> p d t", d=4)[:, :, 0 : 3 * P])
         nc.sync.dma_start(w1w[:], w1t_words[0].rearrange("p k d -> p (k d)").bitcast(I32))
         for q in range(4):
             nc.sync.dma_start(w1s[32 * q : 32 * q + 4, :].bitcast(I32), w1t_scales[0, 4 * q : 4 * q + 4, :].bitcast(I32))
-        nc.sync.dma_start(a_t[:], a.rearrange("(p d) t -> p d t", d=4)[:, :, 0 : 3 * P])
 
         gw = held.tile([P, S], U32, name="gw", align_bytes=64)
         gs = held.tile([P, S], U8, name="gs", align_bytes=64)
@@ -113,7 +113,7 @@ def tile_moe_sub_relu2_kernel(
         gather_words(3 * C + P, S)
         for r in range(2):
             nc.vector.scalar_tensor_tensor(
-                gl[r][:], a_last[:], 0.0, gate_t[r][:, 2 * P : 3 * P].unsqueeze(1).to_broadcast([P, 4, P]), MAX, MULT
+                gl[r][:], a_last[:], 0.0, gate_t[r][:, 3 * P : T].unsqueeze(1).to_broadcast([P, 4, P]), MAX, MULT
             )
 
         products(0, 0, 2 * C, 0)
@@ -133,164 +133,130 @@ def tile_moe_sub_relu2_kernel(
         def turn(dst, src, start, stop):
             nc.tensor.matmul(dst, src, ident[:], start=start, stop=stop, is_transpose=True)
 
-        dh_t = held.tile([P, 2, 4, P], F32, name="dh_t", align_bytes=64)
+        dh_t = held.tile([P, 3, 4, P], F32, name="dh_t", align_bytes=64)
 
-        def main_tokens(j, banks):
-            if len(banks) == 1:
-                whole = bank(banks[0], [P, 2, P], "sums%d" % j)
-                sums = [whole[:, k, :] for k in range(2)]
-            else:
-                sums = [bank(b, [P, P], "sums%d_%d" % (j, b))[:] for b in banks]
-            z = []
+        def gated_sums(j, t0, b):
+            n = 3 - t0
+            sums = bank(b, [P, n, P], "sums%d" % j)
             for r in range(2):
                 if (j, r) == (0, 0):
-                    z.append(gate_t[0][:, 2 * P : 4 * P])
+                    z = gate_t[0][:, 3 * P : 6 * P]
                 else:
-                    z.append(held.tile([P, 2 * P], F32, name="z%d_%d" % (j, r), align_bytes=64)[:])
-                nc.vector.tensor_tensor(z[r], picked(j, r, P, 3 * P), gate_t[r][:, 0 : 2 * P], MULT)
-            if len(banks) == 1:
-                for k in range(2):
-                    for r in range(2):
-                        turn(sums[k], z[r][:, P * k : P * (k + 1)], r == 0, r == 1)
-                nc.scalar.copy(
-                    dh_t[:, :, :, 32 * j : 32 * (j + 1)].rearrange("t k d p -> t k p d"),
-                    whole[:].rearrange("t k (p d) -> t k p d", d=4),
-                )
-            else:
-                for r in range(2):
-                    for k in range(2):
-                        turn(sums[k], z[r][:, P * k : P * (k + 1)], r == 0, r == 1)
-                for k in range(2):
-                    nc.scalar.copy(
-                        dh_t[:, k, :, 32 * j : 32 * (j + 1)].rearrange("t d p -> t p d"),
-                        sums[k].rearrange("t (p d) -> t p d", d=4),
-                    )
+                    z = held.tile([P, n * P], F32, name="z%d_%d" % (j, r), align_bytes=64)[:]
+                nc.vector.tensor_tensor(z, picked(j, r, P * t0, 3 * P), gate_t[r][:, P * t0 : 3 * P], MULT)
+                for k in range(n):
+                    turn(sums[:, k, :], z[:, P * k : P * (k + 1)], (r, k) == (0, 0), (r, k) == (1, n - 1))
+            return lambda: nc.scalar.copy(
+                dh_t[:, t0:3, :, 32 * j : 32 * (j + 1)].rearrange("t k d p -> t k p d"),
+                sums[:].rearrange("t k (p d) -> t k p d", d=4),
+            )
 
-        raw = [held.tile([P, 4, P], F32, name="raw%d" % r, tag=("w2s", "w2w")[r], align_bytes=64) for r in range(2)]
-        gated = held.tile([P, 4, P], F32, name="gated", tag="gated", align_bytes=64)
-        dh_first = held.tile([P, 4, P], F32, name="dh_first", align_bytes=64)
-        turned = {}
+        raw = [held.tile([P, 3, P], F32, name="raw%d" % r, tag=("w2s", "w2w")[r], align_bytes=64) for r in range(2)]
+        gated = held.tile([P, 4, 96], F32, name="gated", align_bytes=64)
+        first_list = [bank(7, [P, 2, P], "first_list0"), bank(6, [P, 1, P], "first_list1")]
+        second_list = bank(0, [P, 3, P], "second_list")
 
-        def first_tokens(r, j, b, width):
-            if b not in turned:
-                turned[b] = bank(b, [P, width, P], "turned%d" % b)
-            nc.scalar.activation(raw[r][:, j, :], picked(j, r, 0, P), COPY)
-            turn(turned[b][:, j % width, :], raw[r][:, j, :], True, True)
+        def first_tokens(r, j):
+            nc.scalar.activation(raw[r][:, j - 1, :], picked(j, r, 0, P), COPY)
+            dst = second_list[:, j - 1, :] if r else first_list[j // 3][:, (j - 1) % 2, :]
+            turn(dst, raw[r][:, j - 1, :], True, True)
 
-        def times_gate(half, b):
+        def times_gate(part, p0, p1):
             nc.scalar.activation(
-                gated[:, :, 64 * half : 64 * (half + 1)],
-                turned[b][:].rearrange("t j (q d) -> t d (j q)", d=4),
+                gated[:, :, p0:p1],
+                first_list[part][:].rearrange("t j (q d) -> t d (j q)", d=4),
                 COPY,
                 scale=gate_col[:, 0:1],
             )
 
         def sum_first():
             nc.vector.scalar_tensor_tensor(
-                dh_first[:],
-                turned[0][:].rearrange("t j (q d) -> t d (j q)", d=4),
+                dh_t[:, 0, :, 32:P],
+                second_list[:].rearrange("t j (q d) -> t d (j q)", d=4),
                 gate_col[:, 1:2],
                 gated[:],
                 MULT,
                 ADD,
             )
 
-        main_tokens(0, (1,))
-        main_tokens(1, (2,))
-        first_tokens(0, 0, 7, 2)
-        first_tokens(0, 1, 7, 2)
-        main_tokens(2, (3,))
-        first_tokens(0, 2, 2, 2)
-        first_tokens(0, 3, 2, 2)
-        main_tokens(3, (5, 6))
+        back = {}
 
-        back = [bank(b, [P, 4, P], "back%d" % tt) for tt, b in enumerate((4, 1))]
+        def turn_back(tt, b):
+            back[tt] = bank(b, [P, 4, P], "back%d" % tt)
+            for d in range(4):
+                turn(back[tt][:, d, :], dh_t[:, tt, d, :], True, True)
+
+        slope = {}
+
+        def lay_slope(tt):
+            slope[tt] = held.tile([P, P, 4], F32, name="slope%d" % tt, align_bytes=64)
+            nc.scalar.activation(
+                slope[tt][:].rearrange("p (c i) d -> p c d i", i=4),
+                a_t[:, :, P * tt : P * (tt + 1)].rearrange("p d (c i) -> p c d i", i=4),
+                RELU,
+            )
+
+        gated_sums(0, 0, 1)()
+        copy_sums = gated_sums(1, 1, 2)
+        for j in range(1, 4):
+            first_tokens(0, j)
+        copy_sums()
+        copy_sums = gated_sums(2, 1, 3)
+        first_tokens(1, 1)
+        first_tokens(1, 2)
+        copy_sums()
+        copy_sums = gated_sums(3, 1, 3)
+        first_tokens(1, 3)
+        copy_sums()
+        turn_back(1, 1)
+        turn_back(2, 2)
+
         z_last = [held.tile([P, 4, P], F32, name="z_last%d" % r, tag="gate%d" % r, align_bytes=64) for r in range(2)]
-        last_sums = [bank(6, [P, 2 * P], "last_sums0")]
-
-        def turn_back(k):
-            for d in range(4):
-                turn(back[1 + k][:, d, :], dh_t[:, k, d, :], True, True)
-
-        def turn_back_first():
-            for d in range(4):
-                turn(back[0][:, d, :], dh_first[:, d, :], True, True)
+        da_last = held.tile([P, 2, P, 2], BF16, name="da_last", align_bytes=64)
 
         def last_tokens(j, dst):
             for r in range(2):
                 nc.vector.tensor_tensor(z_last[r][:, j, :], picked(j, r, 3 * P, T), gl[r][:, j, :], MULT)
                 turn(dst, z_last[r][:, j, :], r == 0, r == 1)
 
-        def round_last(part, p0, p1):
-            nc.scalar.copy(da_last[:, :, p0:p1, :], last_sums[part][:].rearrange("t (p u e) -> t u p e", u=2, e=2))
+        def round_last(sums, p0, p1):
+            nc.scalar.copy(da_last[:, :, p0:p1, :], sums[:].rearrange("t (p u e) -> t u p e", u=2, e=2))
 
-        da_last = held.tile([P, 2, P, 2], BF16, name="da_last", align_bytes=64)
-        turn_back(0)
-        last_tokens(0, last_sums[0][:, 0:P])
-        first_tokens(1, 0, 0, 4)
-        last_tokens(1, last_sums[0][:, P : 2 * P])
-        times_gate(0, 7)
-        first_tokens(1, 1, 0, 4)
-        last_sums.append(bank(7, [P, P], "last_sums1"))
-        last_tokens(2, last_sums[1][:])
-        first_tokens(1, 2, 0, 4)
-        first_tokens(1, 3, 0, 4)
-        times_gate(1, 2)
-        last_sums.append(bank(2, [P, P], "last_sums2"))
-        last_tokens(3, last_sums[2][:])
-        slope_middle = held.tile([P, 2 * P, 4], F32, name="slope_middle", align_bytes=64)
-        nc.vector.tensor_scalar_max(
-            slope_middle[:].rearrange("p (c i) d -> p c d i", i=4),
-            a_t[:, :, P : 3 * P].rearrange("p d (c i) -> p c d i", i=4),
-            0.0,
-        )
-        round_last(0, 0, 64)
-        back.append(bank(6, [P, 4, P], "back2"))
-        turn_back(1)
-        round_last(1, 64, 96)
-        round_last(2, 96, P)
-        slope_first = held.tile([P, P, 4], F32, name="slope_first", tag="w2w", align_bytes=64)
-        nc.scalar.activation(
-            slope_first[:].rearrange("p (c i) d -> p c d i", i=4),
-            a_t[:, :, 0:P].rearrange("p d (c i) -> p c d i", i=4),
-            RELU,
-        )
-        slope = [slope_first[:], slope_middle[:, 0:P, :], slope_middle[:, P : 2 * P, :]]
+        times_gate(0, 0, 64)
+        early_sums = bank(7, [P, 3 * P], "early_sums")
+        for j in range(3):
+            last_tokens(j, early_sums[:, P * j : P * (j + 1)])
+        times_gate(1, 64, 96)
+        late_sums = bank(6, [P, P], "late_sums")
+        last_tokens(3, late_sums[:])
+        lay_slope(1)
+        lay_slope(2)
         sum_first()
-        turn_back_first()
+        turn_back(0, 4)
+        round_last(early_sums, 0, 96)
+        round_last(late_sums, 96, P)
+        lay_slope(0)
 
         groups = ((0, P), (P, 2 * P), (3 * P, P))
-        middle = held.tile([P, 2, 4 * P], BF16, name="middle", tag="gated", align_bytes=64)
-        grouped = [
-            held.tile([P, 4 * P], BF16, name="grouped0", align_bytes=64)[:],
-            middle[:, 0, :],
-            middle[:, 1, :],
-            held.tile([P, 4 * P], BF16, name="grouped3", align_bytes=64)[:],
-        ]
-        wt = bank(3, [P, 2, P], "wt")
+        grouped = [held.tile([P, 4 * n], BF16, name="grouped%d" % t0, align_bytes=64) for t0, n in groups]
+        wt = bank(5, [P, 2, P], "wt")
         words = da_last[:].rearrange("t u p e -> t (u p e)").bitcast(F32)
         for u in range(2):
             turn(wt[:, u, :], words[:, P * u : P * (u + 1)], True, True)
         nc.scalar.copy(
-            grouped[3][:].bitcast(F32).rearrange("p (t u) -> p t u", u=2), wt[:].rearrange("p u t -> p t u")
+            grouped[2][:].bitcast(F32).rearrange("p (t u) -> p t u", u=2), wt[:].rearrange("p u t -> p t u")
         )
 
-        def times_slope(tt):
+        def times_slope(tt, dst):
             nc.vector.tensor_tensor(
-                grouped[tt][:].rearrange("p (t d) -> p t d", d=4),
-                back[tt][:].rearrange("p d t -> p t d"),
-                slope[tt],
-                MULT,
+                dst.rearrange("p (t d) -> p t d", d=4), back[tt][:].rearrange("p d t -> p t d"), slope[tt][:], MULT
             )
 
         def finish(piece, b):
             t0, n = groups[piece]
             codes = held.tile([P, n], U32, name="codes%d" % piece, align_bytes=64)
             scales = held.tile([P, n], U8, name="scales%d" % piece, align_bytes=64)
-            for c0 in range(0, n, P):
-                nc.vector.quantize_mx(
-                    out=codes[:, c0 : c0 + P].bitcast(FP8X4), scales=scales[:, c0 : c0 + P], in_=grouped[(t0 + c0) // P][:]
-                )
+            nc.vector.quantize_mx(out=codes[:].bitcast(FP8X4), scales=scales[:], in_=grouped[piece][:])
             acc = bank(b, [P, n], "acc_out%d" % piece)
             nc.tensor.matmul_mx(
                 out=acc[:],
@@ -305,9 +271,9 @@ def tile_moe_sub_relu2_kernel(
             nc.scalar.activation(res[:], acc[:], COPY, scale=2.0)
             nc.sync.dma_start(out[:, t0 : t0 + n], res[:])
 
-        times_slope(1)
-        times_slope(2)
-        finish(1, 0)
-        times_slope(0)
-        finish(2, 5)
+        times_slope(1, grouped[1][:, 0 : 4 * P])
+        times_slope(2, grouped[1][:, 4 * P : 8 * P])
+        finish(1, 6)
+        times_slope(0, grouped[0][:])
+        finish(2, 7)
         finish(0, 1)

@@ -44,7 +44,8 @@ def tile_moe_sub_relu2_kernel(
         w1s = held.tile([P, K], U8, name="w1s", align_bytes=64)
         gate_t = [held.tile([P, 6 * P], F32, name="gate%d" % r, tag="gate%d" % r, align_bytes=64) for r in range(2)]
         gate_col = held.tile([P, 2], F32, name="gate_col")
-        a_t = held.tile([P, 4, 3 * P], F32, name="a_t")
+        a_t = held.tile([P, 4, 2 * P], F32, name="a_t")
+        a_third = held.tile([P, 4, P], F32, name="a_third", tag="a_third", align_bytes=64)
         a_last = held.tile([P, 4, P], F32, name="a_last", align_bytes=64)
         gl = [held.tile([P, 4, P], F32, name="gl%d" % r, align_bytes=64) for r in range(2)]
         ident = held.tile([P, P], F32, name="ident")
@@ -74,7 +75,9 @@ def tile_moe_sub_relu2_kernel(
         nc.sync.dma_start(pos_t[1][:], pos2)
         with nc.allow_non_contiguous_dma(reason="one gate a partition"):
             nc.sync.dma_start(gate_col[:], gate[:, 0, 0:P].rearrange("r t -> t r"))
-        nc.sync.dma_start(a_t[:], a.rearrange("(p d) t -> p d t", d=4)[:, :, 0 : 3 * P])
+        a_rows = a.rearrange("(p d) t -> p d t", d=4)
+        nc.sync.dma_start(a_third[:], a_rows[:, :, 2 * P : 3 * P])
+        nc.sync.dma_start(a_t[:], a_rows[:, :, 0 : 2 * P])
         nc.sync.dma_start(w1w[:], w1t_words[0].rearrange("p k d -> p (k d)").bitcast(I32))
         for q in range(4):
             nc.sync.dma_start(w1s[32 * q : 32 * q + 4, :].bitcast(I32), w1t_scales[0, 4 * q : 4 * q + 4, :].bitcast(I32))
@@ -192,7 +195,7 @@ def tile_moe_sub_relu2_kernel(
             slope[tt] = held.tile([P, P, 4], F32, name="slope%d" % tt, align_bytes=64)
             nc.scalar.activation(
                 slope[tt][:].rearrange("p (c i) d -> p c d i", i=4),
-                a_t[:, :, P * tt : P * (tt + 1)].rearrange("p d (c i) -> p c d i", i=4),
+                (a_third[:] if tt == 2 else a_t[:, :, P * tt : P * (tt + 1)]).rearrange("p d (c i) -> p c d i", i=4),
                 RELU,
             )
 
@@ -208,16 +211,16 @@ def tile_moe_sub_relu2_kernel(
         copy_sums = gated_sums(3, 1, 3)
         first_tokens(1, 3)
         copy_sums()
-        turn_back(1, 1)
         turn_back(2, 2)
+        turn_back(1, 1)
 
-        z_last = [held.tile([P, 4, P], F32, name="z_last%d" % r, tag="gate%d" % r, align_bytes=64) for r in range(2)]
+        z_last = [held.tile([P, 3, P], F32, name="z_last%d" % r, tag="gate%d" % r, align_bytes=64) for r in range(2)]
         da_last = held.tile([P, 2, P, 2], BF16, name="da_last", align_bytes=64)
 
-        def last_tokens(j, dst):
+        def last_tokens(j, z, dst):
             for r in range(2):
-                nc.vector.tensor_tensor(z_last[r][:, j, :], picked(j, r, 3 * P, T), gl[r][:, j, :], MULT)
-                turn(dst, z_last[r][:, j, :], r == 0, r == 1)
+                nc.vector.tensor_tensor(z[r], picked(j, r, 3 * P, T), gl[r][:, j, :], MULT)
+                turn(dst, z[r], r == 0, r == 1)
 
         def round_last(sums, p0, p1):
             nc.scalar.copy(da_last[:, :, p0:p1, :], sums[:].rearrange("t (p u e) -> t u p e", u=2, e=2))
@@ -225,17 +228,18 @@ def tile_moe_sub_relu2_kernel(
         times_gate(0, 0, 64)
         early_sums = bank(7, [P, 3 * P], "early_sums")
         for j in range(3):
-            last_tokens(j, early_sums[:, P * j : P * (j + 1)])
+            last_tokens(j, [z_last[r][:, j, :] for r in range(2)], early_sums[:, P * j : P * (j + 1)])
         times_gate(1, 64, 96)
-        late_sums = bank(6, [P, P], "late_sums")
-        last_tokens(3, late_sums[:])
-        lay_slope(1)
-        lay_slope(2)
         sum_first()
         turn_back(0, 4)
+        lay_slope(2)
+        late_sums = bank(6, [P, P], "late_sums")
+        z_late = held.tile([P, 2, P], F32, name="z_late", tag="a_third", align_bytes=64)
+        last_tokens(3, [z_late[:, r, :] for r in range(2)], late_sums[:])
+        lay_slope(1)
+        lay_slope(0)
         round_last(early_sums, 0, 96)
         round_last(late_sums, 96, P)
-        lay_slope(0)
 
         groups = ((0, P), (P, 2 * P), (3 * P, P))
         grouped = [held.tile([P, 4 * n], BF16, name="grouped%d" % t0, align_bytes=64) for t0, n in groups]
@@ -271,9 +275,9 @@ def tile_moe_sub_relu2_kernel(
             nc.scalar.activation(res[:], acc[:], COPY, scale=2.0)
             nc.sync.dma_start(out[:, t0 : t0 + n], res[:])
 
-        times_slope(1, grouped[1][:, 0 : 4 * P])
         times_slope(2, grouped[1][:, 4 * P : 8 * P])
-        finish(1, 6)
+        times_slope(1, grouped[1][:, 0 : 4 * P])
         times_slope(0, grouped[0][:])
-        finish(2, 7)
+        finish(1, 6)
         finish(0, 1)
+        finish(2, 7)

from contextlib import ExitStack

import concourse.mybir as mybir
from concourse.masks import make_identity

K, T, E, C, H, N = 128, 512, 4, 256, 512, 512
S = E * C
P = 128
FLOPS = 2 * N * H * S + 2 * H * K * T

F32 = mybir.dt.float32
BF16 = mybir.dt.bfloat16
I32 = mybir.dt.int32
U32 = mybir.dt.uint32
U16 = mybir.dt.uint16
U8 = mybir.dt.uint8
FP8X4 = mybir.dt.float8_e4m3fn_x4
FP4X4 = mybir.dt.float4_e2m1fn_x4
MULT = mybir.AluOpType.mult
MAX = mybir.AluOpType.max
ADD = mybir.AluOpType.add
COPY = mybir.ActivationFunctionType.Copy
RELU = mybir.ActivationFunctionType.Relu


def tile_moe_sub_relu2_kernel(
    tc, dy_words, dy_scales, w2t_words, w2t_scales, w1t_words, w1t_scales, a, gate, offs, pos1, pos2, out
):
    nc = tc.nc
    with ExitStack() as ctx:
        held = ctx.enter_context(tc.tile_pool(name="held", bufs=1))
        psum = ctx.enter_context(tc.psum_pool(name="psum", bufs=1))

        def bank(b, shape, name):
            return psum.tile(shape, F32, name=name, tag="bank%d" % b)

        offs_t = held.tile([P, S // 16], U16, name="offs_t")
        pos_t = [held.tile([P, T // 16], U16, name="pos_t%d" % r) for r in range(2)]
        dyw = held.tile([P, T + 192], I32, name="dyw", align_bytes=64)
        dys = held.tile([P, 2 * T], U8, name="dys", align_bytes=64)
        w2w = held.tile([P, E, 2 * H], U8, name="w2w", tag="w2w", align_bytes=64)
        w2s = held.tile([P, E, H], U8, name="w2s", tag="w2s", align_bytes=64)
        w1w = held.tile([P, K], I32, name="w1w", align_bytes=64)
        w1s = held.tile([P, K], U8, name="w1s", align_bytes=64)
        gate_t = [held.tile([P, 6 * P], F32, name="gate%d" % r, tag="gate%d" % r, align_bytes=64) for r in range(2)]
        gate_col = held.tile([P, 2], F32, name="gate_col")
        a_t = held.tile([P, 4, 2 * P], F32, name="a_t")
        a_third = held.tile([P, 4, P], F32, name="a_third", tag="a_third", align_bytes=64)
        a_last = held.tile([P, 4, P], F32, name="a_last", align_bytes=64)
        gl = [held.tile([P, 4, P], F32, name="gl%d" % r, align_bytes=64) for r in range(2)]
        ident = held.tile([P, P], F32, name="ident")

        nc.sync.dma_start(offs_t[:], offs)
        for q in range(4):
            (nc.sync if q < 2 else nc.scalar).dma_start(
                dys[32 * q : 32 * (q + 1), 0:T].bitcast(I32),
                dy_scales[0, 4 * q : 4 * q + 4, :].bitcast(I32).unsqueeze(0).to_broadcast([8, 4, T // 4]),
            )
        nc.vector.memset(dys[:, T : 2 * T].bitcast(I32), 0)
        nc.vector.memset(dyw[:, T : T + 192], 0)
        nc.scalar.dma_start(dyw[:, 0:T], dy_words[0].rearrange("p t d -> p (t d)").bitcast(I32))
        nc.vector.memset(w2s[:].rearrange("p e c -> p (e c)").bitcast(I32), 0)
        nc.gpsimd.memset(w1s[:].bitcast(I32), 0)
        make_identity(nc, ident[:])
        nc.sync.dma_start(pos_t[0][:], pos1)
        nc.sync.dma_start(w2w[:].bitcast(I32), w2t_words[:, 0].rearrange("e p c -> p e c").bitcast(I32))
        for q in range(4):
            nc.sync.dma_start(
                w2s[32 * q : 32 * q + 4].bitcast(I32),
                w2t_scales[:, 0, 4 * q : 4 * q + 4, :].rearrange("e r c -> r e c").bitcast(I32),
            )
        for r in range(2):
            nc.sync.dma_start(gate_t[r][:, 0:T], gate[r])
        nc.sync.dma_start(a_last[:], a.rearrange("(j p) t -> p j t", p=P)[:, :, 3 * P : T])
        nc.sync.dma_start(pos_t[1][:], pos2)
        with nc.allow_non_contiguous_dma(reason="one gate a partition"):
            nc.sync.dma_start(gate_col[:], gate[:, 0, 0:P].rearrange("r t -> t r"))
        a_rows = a.rearrange("(p d) t -> p d t", d=4)
        nc.sync.dma_start(a_third[:], a_rows[:, :, 2 * P : 3 * P])
        nc.sync.dma_start(a_t[:], a_rows[:, :, 0 : 2 * P])
        nc.sync.dma_start(w1w[:], w1t_words[0].rearrange("p k d -> p (k d)").bitcast(I32))
        for q in range(4):
            nc.sync.dma_start(w1s[32 * q : 32 * q + 4, :].bitcast(I32), w1t_scales[0, 4 * q : 4 * q + 4, :].bitcast(I32))

        gw = held.tile([P, S], U32, name="gw", align_bytes=64)
        gs = held.tile([P, S], U8, name="gs", align_bytes=64)
        y = [held.tile([P, S], F32, name="y%d" % j, align_bytes=64) for j in range(4)]

        def gather_words(s0, s1):
            nc.vector.tensor_copy(gw[:, s0:s1], dyw[:].bitcast(U32).indirect(offs_t[:, s0 // 16 : s1 // 16]))

        def gather_scales(s0, s1):
            nc.vector.tensor_copy(gs[:, s0:s1], dys[:].indirect(offs_t[:, s0 // 16 : s1 // 16]))

        def products(j, s0, s1, b):
            acc = bank(b, [P, s1 - s0], "y%d_%d" % (j, s0))
            for c0 in range(s0, s1, C):
                c1 = min(c0 + C, s1)
                e = c0 // C
                nc.tensor.matmul_mx(
                    out=acc[:, c0 - s0 : c1 - s0],
                    lhsT=w2w[:, e, 2 * P * j : 2 * P * (j + 1)].bitcast(FP4X4),
                    lhsT_scale=w2s[:, e, P * j : P * (j + 1)],
                    rhs=gw[:, c0:c1].bitcast(FP8X4),
                    rhs_scale=gs[:, c0:c1],
                    start=True,
                    stop=True,
                )
            nc.scalar.copy(y[j][:, s0:s1], acc[:])

        gather_scales(0, 2 * C)
        gather_words(0, 2 * C)
        gather_scales(2 * C, S)
        gather_words(2 * C, 3 * C)
        gather_words(3 * C, 3 * C + P)
        gather_words(3 * C + P, S)
        for r in range(2):
            nc.vector.scalar_tensor_tensor(
                gl[r][:], a_last[:], 0.0, gate_t[r][:, 3 * P : T].unsqueeze(1).to_broadcast([P, 4, P]), MAX, MULT
            )

        products(0, 0, 2 * C, 0)
        products(1, 0, 2 * C, 4)
        products(2, 0, 2 * C, 6)
        products(0, 2 * C, 3 * C, 1)
        products(0, 3 * C, 3 * C + P, 2)
        products(0, 3 * C + P, S, 3)
        products(1, 2 * C, S, 5)
        products(2, 2 * C, S, 7)
        products(3, 0, 2 * C, 0)
        products(3, 2 * C, S, 4)

        def picked(j, r, t0, t1):
            return y[j][:].indirect(pos_t[r][:, t0 // 16 : t1 // 16])

        def turn(dst, src, start, stop):
            nc.tensor.matmul(dst, src, ident[:], start=start, stop=stop, is_transpose=True)

        dh_t = held.tile([P, 3, 4, P], F32, name="dh_t", align_bytes=64)

        def gated_sums(j, t0, b):
            n = 3 - t0
            sums = bank(b, [P, n, P], "sums%d" % j)
            for r in range(2):
                if (j, r) == (0, 0):
                    z = gate_t[0][:, 3 * P : 6 * P]
                else:
                    z = held.tile([P, n * P], F32, name="z%d_%d" % (j, r), align_bytes=64)[:]
                nc.vector.tensor_tensor(z, picked(j, r, P * t0, 3 * P), gate_t[r][:, P * t0 : 3 * P], MULT)
                for k in range(n):
                    turn(sums[:, k, :], z[:, P * k : P * (k + 1)], (r, k) == (0, 0), (r, k) == (1, n - 1))
            return lambda: nc.scalar.copy(
                dh_t[:, t0:3, :, 32 * j : 32 * (j + 1)].rearrange("t k d p -> t k p d"),
                sums[:].rearrange("t k (p d) -> t k p d", d=4),
            )

        raw = [held.tile([P, 3, P], F32, name="raw%d" % r, tag=("w2s", "w2w")[r], align_bytes=64) for r in range(2)]
        gated = held.tile([P, 4, 96], F32, name="gated", align_bytes=64)
        first_list = [bank(7, [P, 2, P], "first_list0"), bank(6, [P, 1, P], "first_list1")]
        second_list = bank(0, [P, 3, P], "second_list")

        def first_tokens(r, j):
            nc.scalar.activation(raw[r][:, j - 1, :], picked(j, r, 0, P), COPY)
            dst = second_list[:, j - 1, :] if r else first_list[j // 3][:, (j - 1) % 2, :]
            turn(dst, raw[r][:, j - 1, :], True, True)

        def times_gate(part, p0, p1):
            nc.scalar.activation(
                gated[:, :, p0:p1],
                first_list[part][:].rearrange("t j (q d) -> t d (j q)", d=4),
                COPY,
                scale=gate_col[:, 0:1],
            )

        def sum_first():
            nc.vector.scalar_tensor_tensor(
                dh_t[:, 0, :, 32:P],
                second_list[:].rearrange("t j (q d) -> t d (j q)", d=4),
                gate_col[:, 1:2],
                gated[:],
                MULT,
                ADD,
            )

        back = {}

        def turn_back(tt, b):
            back[tt] = bank(b, [P, 4, P], "back%d" % tt)
            for d in range(4):
                turn(back[tt][:, d, :], dh_t[:, tt, d, :], True, True)

        slope = {}

        def lay_slope(tt):
            slope[tt] = held.tile([P, P, 4], F32, name="slope%d" % tt, align_bytes=64)
            nc.scalar.activation(
                slope[tt][:].rearrange("p (c i) d -> p c d i", i=4),
                (a_third[:] if tt == 2 else a_t[:, :, P * tt : P * (tt + 1)]).rearrange("p d (c i) -> p c d i", i=4),
                RELU,
            )

        gated_sums(0, 0, 1)()
        copy_sums = gated_sums(1, 1, 2)
        for j in range(1, 4):
            first_tokens(0, j)
        copy_sums()
        copy_sums = gated_sums(2, 1, 3)
        first_tokens(1, 1)
        first_tokens(1, 2)
        copy_sums()
        copy_sums = gated_sums(3, 1, 3)
        first_tokens(1, 3)
        copy_sums()
        turn_back(2, 2)
        turn_back(1, 1)

        z_last = [held.tile([P, 3, P], F32, name="z_last%d" % r, tag="gate%d" % r, align_bytes=64) for r in range(2)]
        da_last = held.tile([P, 2, P, 2], BF16, name="da_last", align_bytes=64)

        def last_tokens(j, z, dst):
            for r in range(2):
                nc.vector.tensor_tensor(z[r], picked(j, r, 3 * P, T), gl[r][:, j, :], MULT)
                turn(dst, z[r], r == 0, r == 1)

        def round_last(sums, p0, p1):
            nc.scalar.copy(da_last[:, :, p0:p1, :], sums[:].rearrange("t (p u e) -> t u p e", u=2, e=2))

        times_gate(0, 0, 64)
        early_sums = bank(7, [P, 3 * P], "early_sums")
        for j in range(3):
            last_tokens(j, [z_last[r][:, j, :] for r in range(2)], early_sums[:, P * j : P * (j + 1)])
        times_gate(1, 64, 96)
        sum_first()
        turn_back(0, 4)
        lay_slope(2)
        late_sums = bank(6, [P, P], "late_sums")
        z_late = held.tile([P, 2, P], F32, name="z_late", tag="a_third", align_bytes=64)
        last_tokens(3, [z_late[:, r, :] for r in range(2)], late_sums[:])
        lay_slope(1)
        lay_slope(0)
        round_last(early_sums, 0, 96)
        round_last(late_sums, 96, P)

        groups = ((0, P), (P, 2 * P), (3 * P, P))
        grouped = [held.tile([P, 4 * n], BF16, name="grouped%d" % t0, align_bytes=64) for t0, n in groups]
        wt = bank(5, [P, 2, P], "wt")
        words = da_last[:].rearrange("t u p e -> t (u p e)").bitcast(F32)
        for u in range(2):
            turn(wt[:, u, :], words[:, P * u : P * (u + 1)], True, True)
        nc.scalar.copy(
            grouped[2][:].bitcast(F32).rearrange("p (t u) -> p t u", u=2), wt[:].rearrange("p u t -> p t u")
        )

        def times_slope(tt, dst):
            nc.vector.tensor_tensor(
                dst.rearrange("p (t d) -> p t d", d=4), back[tt][:].rearrange("p d t -> p t d"), slope[tt][:], MULT
            )

        def finish(piece, b):
            t0, n = groups[piece]
            codes = held.tile([P, n], U32, name="codes%d" % piece, align_bytes=64)
            scales = held.tile([P, n], U8, name="scales%d" % piece, align_bytes=64)
            nc.vector.quantize_mx(out=codes[:].bitcast(FP8X4), scales=scales[:], in_=grouped[piece][:])
            acc = bank(b, [P, n], "acc_out%d" % piece)
            nc.tensor.matmul_mx(
                out=acc[:],
                lhsT=w1w[:].bitcast(FP8X4),
                lhsT_scale=w1s[:],
                rhs=codes[:].bitcast(FP8X4),
                rhs_scale=scales[:],
                start=True,
                stop=True,
            )
            res = held.tile([P, n], F32, name="res%d" % piece)
            nc.scalar.activation(res[:], acc[:], COPY, scale=2.0)
            nc.sync.dma_start(out[:, t0 : t0 + n], res[:])

        times_slope(2, grouped[1][:, 4 * P : 8 * P])
        times_slope(1, grouped[1][:, 0 : 4 * P])
        times_slope(0, grouped[0][:])
        finish(1, 6)
        finish(0, 1)
        finish(2, 7)
